import numpy as np
import ml_dtypes


def mxq(x, axis, fmt="e4m3"):
    dtype, down = {"e4m3": (ml_dtypes.float8_e4m3fn, 7), "e5m2": (ml_dtypes.float8_e5m2, 14)}[fmt]
    v = np.moveaxis(np.asarray(x, np.float32).astype(ml_dtypes.bfloat16).astype(np.float64), axis, -1)
    blocks = v.reshape(v.shape[:-1] + (-1, 32))
    amax = np.abs(blocks).max(-1, keepdims=True)
    byte = np.maximum(np.where(amax > 0, np.frexp(amax)[1] - 1 + 127, 0) - down, 1)
    scale = np.exp2(byte - 127.0)
    codes = (blocks / scale).astype(np.float32).astype(dtype).astype(np.float64)
    return np.moveaxis((codes * scale).reshape(v.shape), -1, axis)


WIDE = False


def mx_kscale(k):
    if not WIDE:
        return np.ones(k)
    levels = np.array([10, -10, 5, -5, 0])
    if k % 512:
        return np.exp2(np.random.permutation(np.resize(levels, k // 32))).repeat(32)
    a = np.empty((k // 512, 16))
    for p in range(k // 512):
        a[p, :8] = np.random.permutation(np.resize(levels, 8))
        for g in range(8):
            far = levels[np.abs(levels - a[p, g]) >= 10]
            a[p, g + 8] = far[np.random.randint(len(far))]
    return np.exp2(a.ravel()).repeat(32)


def f64(x):
    return np.asarray(x).astype(np.float64)


def striped(idx):
    return np.tile(idx.reshape(-1, 16).T, (8, 1)).astype(np.uint16)


def unstriped(offs):
    return offs[:16].T.reshape(-1).astype(np.int64)


def pack_weight(w):
    k, n = w.shape
    w = f64(np.asarray(w, np.float32).astype(ml_dtypes.bfloat16)).reshape(k // 32, 32, n)
    amax = np.abs(w).max(1)
    byte = np.clip(np.where(amax > 0, np.frexp(amax)[1] - 1 + 127 - 7, 1), 1, 254)
    scaled = (w * np.exp2(127.0 - byte)[:, None, :]).reshape(k, n).astype(np.float32)
    words = np.ascontiguousarray(scaled.reshape(k // 512, 128, 4, n).transpose(0, 1, 3, 2)).astype(ml_dtypes.float8_e4m3fn).view(np.uint8)
    return words, np.ascontiguousarray(byte.astype(np.uint8).reshape(k // 512, 16, n))


def unpack_weight(words, scales):
    g, p, n, _ = words.shape
    vals = np.ascontiguousarray(words).view(ml_dtypes.float8_e4m3fn).astype(np.float64) * np.repeat(np.exp2(scales.astype(np.float64) - 127.0), 8, axis=1)[..., None]
    return vals.transpose(0, 1, 3, 2).reshape(g * 512, n)


K, T, D, S, V, R, N = 1024, 2048, 7, 1792, 256, 8, 128


def setup_inputs():
    n = np.random.standard_normal
    s = mx_kscale(K)[:, None]
    packed = pack_weight(n((K, T)) * s)
    return {
        "x_words": packed[0],
        "x_scales": packed[1],
        "w": (n((D, K, N)) / np.sqrt(D * K) / s[None]).astype(np.float32),
        "b": (0.3 * n((N, 1))).astype(np.float32),
        "offs": striped(np.concatenate([R * np.arange(V) + np.random.randint(0, R, V) for _ in range(D)])),
    }


def reference(x_words, x_scales, w, b, offs):
    idx = unstriped(offs)
    xq = unpack_weight(x_words, x_scales)[:, idx]
    wq = mxq(f64(w), 1, "e4m3")
    y = sum(wq[d].T @ xq[:, d * V:(d + 1) * V] for d in range(D))
    y = y + f64(b)
    return y

@@ -1,0 +1,123 @@
+from contextlib import ExitStack
+
+import concourse.mybir as mybir
+
+K, T, TAPS, V, M = 1024, 2048, 7, 256, 128
+S = TAPS * V
+P = 128
+PACK = 4
+K_PASS = P * PACK
+PASSES = K // K_PASS
+FLOPS = 2 * S * K * M
+
+F32 = mybir.dt.float32
+BF16 = mybir.dt.bfloat16
+I32 = mybir.dt.int32
+U32 = mybir.dt.uint32
+U16 = mybir.dt.uint16
+U8 = mybir.dt.uint8
+FP8X4 = mybir.dt.float8_e4m3fn_x4
+
+W_LOADS = [(0, 0, 1), (0, 1, 3), (0, 3, 5), (0, 5, 7), (1, 0, 2), (1, 2, 4), (1, 4, 5), (1, 5, 6), (1, 6, 7)]
+GATHER_TAPS = [(0, 2), (2, 4), (4, 7)]
+DMA_ORDER = [("w", 0), ("s", 0), ("x", 0), ("b", 0), ("w", 1), ("w", 2), ("x", 1), ("w", 3), ("w", 4), ("w", 5), ("w", 6), ("w", 7), ("w", 8)]
+VEC_ORDER = [("s", 0), ("s", 1), ("s", 2), ("q", 0), ("x0", 0), ("x0", 1), ("x0", 2), ("q", 1), ("q", 2), ("x1", 0), ("x1", 1), ("q", 3), ("x1", 2), ("q", 4), ("q", 5), ("q", 6), ("q", 7), ("q", 8)]
+
+
+def tile_picked_deform_lin_bias_def_p_kernel(tc, x_words, x_scales, w, b, offs, out):
+    nc = tc.nc
+    with ExitStack() as ctx:
+        keep = ctx.enter_context(tc.tile_pool(name="keep", bufs=1))
+        psum = ctx.enter_context(tc.psum_pool(name="psum", bufs=1))
+
+        offsets = keep.tile([P, S // 16], U16, name="offsets")
+        nc.sync.dma_start(offsets[:], offs)
+
+        word_win = [keep.tile([P, T], I32, name="word_win%d" % o, align_bytes=64) for o in range(PASSES)]
+        scale_win = keep.tile([P, T], U8, name="scale_win", align_bytes=64)
+        x_codes = [keep.tile([P, S], U32, name="x_codes%d" % o, align_bytes=64) for o in range(PASSES)]
+        x_scale = keep.tile([P, S], U8, name="x_scale", align_bytes=64)
+        bias = keep.tile([P, 1], F32, name="bias")
+        w_raw, w_bf, w_codes, w_scale = [], [], [], []
+        for i, (o, d0, d1) in enumerate(W_LOADS):
+            n = d1 - d0
+            w_raw.append(keep.tile([P, n, PACK * M], F32, name="w_raw%d" % i, align_bytes=64))
+            w_bf.append(keep.tile([P, n, PACK * M], BF16, name="w_bf%d" % i, align_bytes=64))
+            w_codes.append(keep.tile([P, n * M], U32, name="w_codes%d" % i, align_bytes=64))
+            w_scale.append(keep.tile([P, n * M], U8, name="w_scale%d" % i, align_bytes=64))
+        acc = psum.tile([M, V], F32, name="acc")
+
+        nc.vector.memset(scale_win[:].bitcast(I32), 0)
+
+        def load_scales(eng):
+            for q in range(4):
+                eng.dma_start(
+                    out=scale_win[32 * q : 32 * q + 4 * PASSES, :].bitcast(I32),
+                    in_=x_scales[:, 4 * q : 4 * q + 4, :].bitcast(I32),
+                )
+
+        def load_words(o):
+            nc.sync.dma_start(out=word_win[o][:], in_=x_words[o].rearrange("p c r -> p (c r)").bitcast(I32))
+
+        def load_w(i):
+            o, d0, d1 = W_LOADS[i]
+            nc.sync.dma_start(
+                out=w_raw[i][:],
+                in_=w[d0:d1, o * K_PASS : (o + 1) * K_PASS, :].rearrange("d (p j) m -> p d (j m)", j=PACK),
+            )
+
+        def cast_w(i):
+            o, d0, d1 = W_LOADS[i]
+            for u in range(d1 - d0):
+                nc.scalar.copy(
+                    out=w_bf[i][:, u, :].rearrange("p (c i t) -> p c t i", i=4, t=PACK),
+                    in_=w_raw[i][:, u, :].rearrange("p (t c i) -> p c t i", i=4, t=PACK),
+                )
+
+        def quantize_w(i):
+            nc.vector.quantize_mx(
+                out=w_codes[i][:].bitcast(FP8X4),
+                scales=w_scale[i][:],
+                in_=w_bf[i][:].rearrange("p u c -> p (u c)"),
+            )
+
+        def gather(dst, window, g):
+            d0, d1 = GATHER_TAPS[g]
+            nc.vector.tensor_copy(dst[:, d0 * V : d1 * V], window.indirect(offsets[:, d0 * V // 16 : d1 * V // 16]))
+
+        for kind, i in DMA_ORDER:
+            if kind == "x":
+                load_words(i)
+            elif kind == "w":
+                load_w(i)
+            elif kind == "s":
+                load_scales(nc.sync)
+            else:
+                nc.scalar.dma_start(out=bias[:], in_=b)
+        for i in range(len(W_LOADS)):
+            cast_w(i)
+        for kind, i in VEC_ORDER:
+            if kind == "x0":
+                gather(x_codes[0], word_win[0][:].bitcast(U32), i)
+            elif kind == "x1":
+                gather(x_codes[1], word_win[1][:].bitcast(U32), i)
+            elif kind == "s":
+                gather(x_scale, scale_win[:], i)
+            else:
+                quantize_w(i)
+
+        units = [(i, o, d, d - d0) for i, (o, d0, d1) in enumerate(W_LOADS) for d in range(d0, d1)]
+        for n, (i, o, d, u) in enumerate(units):
+            nc.tensor.matmul_mx(
+                out=acc[:],
+                lhsT=w_codes[i][:, u * M : (u + 1) * M].bitcast(FP8X4),
+                lhsT_scale=w_scale[i][:, u * M : (u + 1) * M],
+                rhs=x_codes[o][:, d * V : (d + 1) * V].bitcast(FP8X4),
+                rhs_scale=x_scale[4 * o :, d * V : (d + 1) * V],
+                start=(n == 0),
+                stop=(n == len(units) - 1),
+            )
+
+        result = keep.tile([M, V], F32, name="result")
+        nc.vector.tensor_scalar_add(result[:], acc[:], bias[:])
+        nc.sync.dma_start(out=out, in_=result[:])

@@ -8,6 +8,11 @@ P = 128
 PACK = 4
 K_PASS = P * PACK
 PASSES = K // K_PASS
+UNITS = PASSES * TAPS
+PARTS = 2
+PART = V // PARTS
+UNIT = [(0, 0), (1, 0), (0, 1), (0, 2), (0, 3), (0, 4), (0, 5), (1, 1), (1, 2), (1, 3), (1, 4), (1, 5), (0, 6), (1, 6)]
+MM_ORDER = [1, 0, 2, 3, 4, 5, 6, 7, 8, 9, 10, 11, 12, 13]
 FLOPS = 2 * S * K * M
 
 F32 = mybir.dt.float32
@@ -18,10 +23,8 @@ U16 = mybir.dt.uint16
 U8 = mybir.dt.uint8
 FP8X4 = mybir.dt.float8_e4m3fn_x4
 
-W_LOADS = [(0, 0, 1), (0, 1, 3), (0, 3, 5), (0, 5, 7), (1, 0, 2), (1, 2, 4), (1, 4, 5), (1, 5, 6), (1, 6, 7)]
-GATHER_TAPS = [(0, 2), (2, 4), (4, 7)]
-DMA_ORDER = [("w", 0), ("s", 0), ("x", 0), ("b", 0), ("w", 1), ("w", 2), ("x", 1), ("w", 3), ("w", 4), ("w", 5), ("w", 6), ("w", 7), ("w", 8)]
-VEC_ORDER = [("s", 0), ("s", 1), ("s", 2), ("q", 0), ("x0", 0), ("x0", 1), ("x0", 2), ("q", 1), ("q", 2), ("x1", 0), ("x1", 1), ("q", 3), ("x1", 2), ("q", 4), ("q", 5), ("q", 6), ("q", 7), ("q", 8)]
+DMA_ORDER = [("b", 0, 0), ("s", 0, 0), ("x", 0, 0), ("w", 0, 2), ("w", 2, 4), ("w", 4, 6), ("w", 6, 7), ("x", 1, 0), ("w", 7, 9), ("w", 9, 11), ("w", 11, 12), ("w", 12, 13), ("w", 13, 14)]
+VEC_ORDER = [("s", 0, 1024), ("s", 1024, 1792), ("x0", 0, 1024), ("x0", 1024, 1792), ("q", 0, 4), ("q", 4, 6), ("q", 6, 7), ("x1", 0, 768), ("x1", 768, 1792), ("q", 7, 9), ("q", 9, 11), ("q", 11, 13), ("q", 13, 14)]
 
 
 def tile_picked_deform_lin_bias_def_p_kernel(tc, x_words, x_scales, w, b, offs, out):
@@ -38,20 +41,18 @@ def tile_picked_deform_lin_bias_def_p_kernel(tc, x_words, x_scales, w, b, offs, 
         x_codes = [keep.tile([P, S], U32, name="x_codes%d" % o, align_bytes=64) for o in range(PASSES)]
         x_scale = keep.tile([P, S], U8, name="x_scale", align_bytes=64)
         bias = keep.tile([P, 1], F32, name="bias")
-        w_raw, w_bf, w_codes, w_scale = [], [], [], []
-        for i, (o, d0, d1) in enumerate(W_LOADS):
-            n = d1 - d0
-            w_raw.append(keep.tile([P, n, PACK * M], F32, name="w_raw%d" % i, align_bytes=64))
-            w_bf.append(keep.tile([P, n, PACK * M], BF16, name="w_bf%d" % i, align_bytes=64))
-            w_codes.append(keep.tile([P, n * M], U32, name="w_codes%d" % i, align_bytes=64))
-            w_scale.append(keep.tile([P, n * M], U8, name="w_scale%d" % i, align_bytes=64))
-        acc = psum.tile([M, V], F32, name="acc")
+        w_raw = keep.tile([P, UNITS, K_PASS], F32, name="w_raw", align_bytes=64)
+        w_bf = keep.tile([P, UNITS * K_PASS], BF16, name="w_bf", align_bytes=64)
+        w_codes = keep.tile([P, UNITS * M], U32, name="w_codes", align_bytes=64)
+        w_scale = keep.tile([P, UNITS * M], U8, name="w_scale", align_bytes=64)
+        acc = [psum.tile([M, PART], F32, name="acc%d" % h) for h in range(PARTS)]
 
-        nc.vector.memset(scale_win[:].bitcast(I32), 0)
+        nc.gpsimd.memset(scale_win[:, : T // 2].bitcast(I32), 0)
+        nc.vector.memset(scale_win[:, T // 2 :].bitcast(I32), 0)
 
-        def load_scales(eng):
+        def load_scales():
             for q in range(4):
-                eng.dma_start(
+                nc.sync.dma_start(
                     out=scale_win[32 * q : 32 * q + 4 * PASSES, :].bitcast(I32),
                     in_=x_scales[:, 4 * q : 4 * q + 4, :].bitcast(I32),
                 )
@@ -59,65 +60,66 @@ def tile_picked_deform_lin_bias_def_p_kernel(tc, x_words, x_scales, w, b, offs, 
         def load_words(o):
             nc.sync.dma_start(out=word_win[o][:], in_=x_words[o].rearrange("p c r -> p (c r)").bitcast(I32))
 
-        def load_w(i):
-            o, d0, d1 = W_LOADS[i]
-            nc.sync.dma_start(
-                out=w_raw[i][:],
-                in_=w[d0:d1, o * K_PASS : (o + 1) * K_PASS, :].rearrange("d (p j) m -> p d (j m)", j=PACK),
+        def load_w(u0, u1):
+            o, d = UNIT[u0]
+            if UNIT[u1 - 1][1] == d and u1 - u0 == PASSES:
+                rows = w[d].rearrange("(o p j) m -> p o (j m)", p=P, j=PACK)
+            else:
+                rows = w[d : d + u1 - u0, o * K_PASS : (o + 1) * K_PASS, :].rearrange("d (p j) m -> p d (j m)", j=PACK)
+            nc.sync.dma_start(out=w_raw[:, u0:u1, :], in_=rows)
+
+        def cast_w(u):
+            nc.scalar.copy(
+                out=w_bf[:, u * K_PASS : (u + 1) * K_PASS].rearrange("p (c i t) -> p c t i", i=4, t=PACK),
+                in_=w_raw[:, u, :].rearrange("p (t c i) -> p c t i", i=4, t=PACK),
             )
 
-        def cast_w(i):
-            o, d0, d1 = W_LOADS[i]
-            for u in range(d1 - d0):
-                nc.scalar.copy(
-                    out=w_bf[i][:, u, :].rearrange("p (c i t) -> p c t i", i=4, t=PACK),
-                    in_=w_raw[i][:, u, :].rearrange("p (t c i) -> p c t i", i=4, t=PACK),
-                )
-
-        def quantize_w(i):
+        def quantize_w(u0, u1):
             nc.vector.quantize_mx(
-                out=w_codes[i][:].bitcast(FP8X4),
-                scales=w_scale[i][:],
-                in_=w_bf[i][:].rearrange("p u c -> p (u c)"),
+                out=w_codes[:, u0 * M : u1 * M].bitcast(FP8X4),
+                scales=w_scale[:, u0 * M : u1 * M],
+                in_=w_bf[:, u0 * K_PASS : u1 * K_PASS],
             )
 
-        def gather(dst, window, g):
-            d0, d1 = GATHER_TAPS[g]
-            nc.vector.tensor_copy(dst[:, d0 * V : d1 * V], window.indirect(offsets[:, d0 * V // 16 : d1 * V // 16]))
+        def gather(dst, window, e0, e1):
+            nc.vector.tensor_copy(dst[:, e0:e1], window.indirect(offsets[:, e0 // 16 : e1 // 16]))
 
-        for kind, i in DMA_ORDER:
+        for kind, i, j in DMA_ORDER:
             if kind == "x":
                 load_words(i)
             elif kind == "w":
-                load_w(i)
+                load_w(i, j)
             elif kind == "s":
-                load_scales(nc.sync)
+                load_scales()
             else:
-                nc.scalar.dma_start(out=bias[:], in_=b)
-        for i in range(len(W_LOADS)):
-            cast_w(i)
-        for kind, i in VEC_ORDER:
+                nc.sync.dma_start(out=bias[:], in_=b)
+        for u in range(UNITS):
+            cast_w(u)
+        for kind, i, j in VEC_ORDER:
             if kind == "x0":
-                gather(x_codes[0], word_win[0][:].bitcast(U32), i)
+                gather(x_codes[0], word_win[0][:].bitcast(U32), i, j)
             elif kind == "x1":
-                gather(x_codes[1], word_win[1][:].bitcast(U32), i)
+                gather(x_codes[1], word_win[1][:].bitcast(U32), i, j)
             elif kind == "s":
-                gather(x_scale, scale_win[:], i)
+                gather(x_scale, scale_win[:], i, j)
             else:
-                quantize_w(i)
+                quantize_w(i, j)
 
-        units = [(i, o, d, d - d0) for i, (o, d0, d1) in enumerate(W_LOADS) for d in range(d0, d1)]
-        for n, (i, o, d, u) in enumerate(units):
-            nc.tensor.matmul_mx(
-                out=acc[:],
-                lhsT=w_codes[i][:, u * M : (u + 1) * M].bitcast(FP8X4),
-                lhsT_scale=w_scale[i][:, u * M : (u + 1) * M],
-                rhs=x_codes[o][:, d * V : (d + 1) * V].bitcast(FP8X4),
-                rhs_scale=x_scale[4 * o :, d * V : (d + 1) * V],
-                start=(n == 0),
-                stop=(n == len(units) - 1),
-            )
-
-        result = keep.tile([M, V], F32, name="result")
-        nc.vector.tensor_scalar_add(result[:], acc[:], bias[:])
-        nc.sync.dma_start(out=out, in_=result[:])
+        for n, u in enumerate(MM_ORDER):
+            o, d = UNIT[u]
+            for h in range(PARTS):
+                cols = slice(d * V + h * PART, d * V + (h + 1) * PART)
+                nc.tensor.matmul_mx(
+                    out=acc[h][:],
+                    lhsT=w_codes[:, u * M : (u + 1) * M].bitcast(FP8X4),
+                    lhsT_scale=w_scale[:, u * M : (u + 1) * M],
+                    rhs=x_codes[o][:, cols].bitcast(FP8X4),
+                    rhs_scale=x_scale[4 * o :, cols],
+                    start=(n == 0),
+                    stop=(n == UNITS - 1),
+                )
+        result = [keep.tile([M, PART], F32, name="result%d" % h) for h in range(PARTS)]
+        nc.scalar.activation(result[0][:], acc[0][:], mybir.ActivationFunctionType.Identity, bias=bias[:])
+        nc.scalar.dma_start(out=out[:, :PART], in_=result[0][:])
+        nc.vector.tensor_scalar_add(result[1][:], acc[1][:], bias[:])
+        nc.sync.dma_start(out=out[:, PART:], in_=result[1][:])

@@ -11,7 +11,7 @@ PASSES = K // K_PASS
 UNITS = PASSES * TAPS
 PARTS = 2
 PART = V // PARTS
-UNIT = [(0, 0), (1, 0), (0, 1), (0, 2), (0, 3), (0, 4), (0, 5), (1, 1), (1, 2), (1, 3), (1, 4), (1, 5), (0, 6), (1, 6)]
+UNIT = [(0, 0), (1, 0), (0, 1), (0, 2), (0, 3), (0, 4), (0, 5), (0, 6), (1, 1), (1, 2), (1, 3), (1, 4), (1, 5), (1, 6)]
 MM_ORDER = [1, 0, 2, 3, 4, 5, 6, 7, 8, 9, 10, 11, 12, 13]
 FLOPS = 2 * S * K * M
 
@@ -23,8 +23,8 @@ U16 = mybir.dt.uint16
 U8 = mybir.dt.uint8
 FP8X4 = mybir.dt.float8_e4m3fn_x4
 
-DMA_ORDER = [("b", 0, 0), ("s", 0, 0), ("x", 0, 0), ("w", 0, 2), ("w", 2, 4), ("w", 4, 6), ("w", 6, 7), ("x", 1, 0), ("w", 7, 9), ("w", 9, 11), ("w", 11, 12), ("w", 12, 13), ("w", 13, 14)]
-VEC_ORDER = [("s", 0, 1024), ("s", 1024, 1792), ("x0", 0, 1024), ("x0", 1024, 1792), ("q", 0, 4), ("q", 4, 6), ("q", 6, 7), ("x1", 0, 768), ("x1", 768, 1792), ("q", 7, 9), ("q", 9, 11), ("q", 11, 13), ("q", 13, 14)]
+DMA_ORDER = [("b", 0, 0), ("s", 0, 0), ("x", 0, 0), ("w", 0, 2), ("w", 2, 4), ("w", 4, 6), ("x", 1, 0), ("w", 6, 8), ("w", 8, 10), ("w", 10, 12), ("w", 12, 13), ("w", 13, 14)]
+VEC_ORDER = [("s", 0, 1024), ("s", 1024, 1792), ("x0", 0, 1024), ("x0", 1024, 1792), ("q", 0, 4), ("q", 4, 6), ("x1", 0, 768), ("x1", 768, 1792), ("q", 6, 8), ("q", 8, 10), ("q", 10, 12), ("q", 12, 13), ("q", 13, 14)]
 
 
 def tile_picked_deform_lin_bias_def_p_kernel(tc, x_words, x_scales, w, b, offs, out):
@@ -47,15 +47,20 @@ def tile_picked_deform_lin_bias_def_p_kernel(tc, x_words, x_scales, w, b, offs, 
         w_scale = keep.tile([P, UNITS * M], U8, name="w_scale", align_bytes=64)
         acc = [psum.tile([M, PART], F32, name="acc%d" % h) for h in range(PARTS)]
 
-        nc.gpsimd.memset(scale_win[:, : T // 2].bitcast(I32), 0)
-        nc.vector.memset(scale_win[:, T // 2 :].bitcast(I32), 0)
+        nc.vector.memset(scale_win[:].bitcast(I32), 0)
 
         def load_scales():
-            for q in range(4):
+            for q in range(3):
                 nc.sync.dma_start(
                     out=scale_win[32 * q : 32 * q + 4 * PASSES, :].bitcast(I32),
                     in_=x_scales[:, 4 * q : 4 * q + 4, :].bitcast(I32),
                 )
+            for o in range(PASSES):
+                for q in range(3, 4):
+                    nc.sync.dma_start(
+                        out=scale_win[32 * q + 4 * o : 32 * q + 4 * o + 4, :].bitcast(I32),
+                        in_=x_scales[o, 4 * q : 4 * q + 4, :].bitcast(I32),
+                    )
 
         def load_words(o):
             nc.sync.dma_start(out=word_win[o][:], in_=x_words[o].rearrange("p c r -> p (c r)").bitcast(I32))

@@ -11,7 +11,7 @@ PASSES = K // K_PASS
 UNITS = PASSES * TAPS
 PARTS = 2
 PART = V // PARTS
-UNIT = [(0, 0), (1, 0), (0, 1), (0, 2), (0, 3), (0, 4), (0, 5), (0, 6), (1, 1), (1, 2), (1, 3), (1, 4), (1, 5), (1, 6)]
+UNIT = [(0, 0), (1, 0), (0, 1), (0, 2), (0, 3), (0, 4), (0, 5), (1, 1), (1, 2), (1, 3), (1, 4), (1, 5), (0, 6), (1, 6)]
 MM_ORDER = [1, 0, 2, 3, 4, 5, 6, 7, 8, 9, 10, 11, 12, 13]
 FLOPS = 2 * S * K * M
 
@@ -23,8 +23,8 @@ U16 = mybir.dt.uint16
 U8 = mybir.dt.uint8
 FP8X4 = mybir.dt.float8_e4m3fn_x4
 
-DMA_ORDER = [("b", 0, 0), ("s", 0, 0), ("x", 0, 0), ("w", 0, 2), ("w", 2, 4), ("w", 4, 6), ("x", 1, 0), ("w", 6, 8), ("w", 8, 10), ("w", 10, 12), ("w", 12, 13), ("w", 13, 14)]
-VEC_ORDER = [("s", 0, 1024), ("s", 1024, 1792), ("x0", 0, 1024), ("x0", 1024, 1792), ("q", 0, 4), ("q", 4, 6), ("x1", 0, 768), ("x1", 768, 1792), ("q", 6, 8), ("q", 8, 10), ("q", 10, 12), ("q", 12, 13), ("q", 13, 14)]
+DMA_ORDER = [("b", 0, 0), ("s", 0, 0), ("x", 0, 0), ("w", 0, 2), ("w", 2, 4), ("w", 4, 6), ("w", 6, 7), ("x", 1, 0), ("w", 7, 8), ("w", 8, 9), ("w", 9, 10), ("w", 10, 11), ("w", 11, 12), ("w", 12, 13), ("w", 13, 14)]
+VEC_ORDER = [("s", 0, 1024), ("s", 1024, 1792), ("x0", 0, 1024), ("x0", 1024, 1792), ("q", 0, 4), ("q", 4, 6), ("q", 6, 7), ("x1", 0, 768), ("x1", 768, 1792), ("q", 7, 9), ("q", 9, 11), ("q", 11, 13), ("q", 13, 14)]
 
 
 def tile_picked_deform_lin_bias_def_p_kernel(tc, x_words, x_scales, w, b, offs, out):

@@ -8,12 +8,18 @@ P = 128
 PACK = 4
 K_PASS = P * PACK
 PASSES = K // K_PASS
-UNITS = PASSES * TAPS
-PARTS = 2
-PART = V // PARTS
-UNIT = [(0, 0), (1, 0), (0, 1), (0, 2), (0, 3), (0, 4), (0, 5), (1, 1), (1, 2), (1, 3), (1, 4), (1, 5), (0, 6), (1, 6)]
-MM_ORDER = [1, 0, 2, 3, 4, 5, 6, 7, 8, 9, 10, 11, 12, 13]
+QUADRANT = 32
+SCALE_ROWS = 4
+LIST_ROWS = 16
+LINE = 4
+HALF = V // 2
 FLOPS = 2 * S * K * M
+
+EARLY = [(0, 0), (1, 0)] + [(0, d) for d in range(1, TAPS - 1)]
+LATE = [(1, d) for d in range(1, TAPS - 1)] + [(0, TAPS - 1), (1, TAPS - 1)]
+PIECES = EARLY + LATE
+FIRST_CUT = 4 * V
+FIRST_CUT_PASS_1 = 3 * V
 
 F32 = mybir.dt.float32
 BF16 = mybir.dt.bfloat16
@@ -23,108 +29,110 @@ U16 = mybir.dt.uint16
 U8 = mybir.dt.uint8
 FP8X4 = mybir.dt.float8_e4m3fn_x4
 
-DMA_ORDER = [("b", 0, 0), ("s", 0, 0), ("x", 0, 0), ("w", 0, 2), ("w", 2, 4), ("w", 4, 6), ("w", 6, 7), ("x", 1, 0), ("w", 7, 8), ("w", 8, 9), ("w", 9, 10), ("w", 10, 11), ("w", 11, 12), ("w", 12, 13), ("w", 13, 14)]
-VEC_ORDER = [("s", 0, 1024), ("s", 1024, 1792), ("x0", 0, 1024), ("x0", 1024, 1792), ("q", 0, 4), ("q", 4, 6), ("q", 6, 7), ("x1", 0, 768), ("x1", 768, 1792), ("q", 7, 9), ("q", 9, 11), ("q", 11, 13), ("q", 13, 14)]
-
 
 def tile_picked_deform_lin_bias_def_p_kernel(tc, x_words, x_scales, w, b, offs, out):
     nc = tc.nc
+    n_early, n_pieces = len(EARLY), len(PIECES)
     with ExitStack() as ctx:
         keep = ctx.enter_context(tc.tile_pool(name="keep", bufs=1))
         psum = ctx.enter_context(tc.psum_pool(name="psum", bufs=1))
 
-        offsets = keep.tile([P, S // 16], U16, name="offsets")
-        nc.sync.dma_start(offsets[:], offs)
-
+        offsets = keep.tile([P, S // LIST_ROWS], U16, name="offsets")
         word_win = [keep.tile([P, T], I32, name="word_win%d" % o, align_bytes=64) for o in range(PASSES)]
         scale_win = keep.tile([P, T], U8, name="scale_win", align_bytes=64)
         x_codes = [keep.tile([P, S], U32, name="x_codes%d" % o, align_bytes=64) for o in range(PASSES)]
         x_scale = keep.tile([P, S], U8, name="x_scale", align_bytes=64)
         bias = keep.tile([P, 1], F32, name="bias")
-        w_raw = keep.tile([P, UNITS, K_PASS], F32, name="w_raw", align_bytes=64)
-        w_bf = keep.tile([P, UNITS * K_PASS], BF16, name="w_bf", align_bytes=64)
-        w_codes = keep.tile([P, UNITS * M], U32, name="w_codes", align_bytes=64)
-        w_scale = keep.tile([P, UNITS * M], U8, name="w_scale", align_bytes=64)
-        acc = [psum.tile([M, PART], F32, name="acc%d" % h) for h in range(PARTS)]
+        w_raw = keep.tile([P, n_pieces, K_PASS], F32, name="w_raw", align_bytes=64)
+        w_bf = keep.tile([P, n_pieces * K_PASS], BF16, name="w_bf", align_bytes=64)
+        w_codes = keep.tile([P, n_pieces * M], U32, name="w_codes", align_bytes=64)
+        w_scale = keep.tile([P, n_pieces * M], U8, name="w_scale", align_bytes=64)
+        acc = [psum.tile([M, HALF], F32, name="acc%d" % h) for h in range(2)]
 
-        nc.vector.memset(scale_win[:].bitcast(I32), 0)
+        def piece_rows(u):
+            o, d = PIECES[u]
+            return w[d, o * K_PASS : (o + 1) * K_PASS, :].rearrange("(p t) m -> p (t m)", t=PACK)
 
-        def load_scales():
-            for q in range(3):
-                nc.sync.dma_start(
-                    out=scale_win[32 * q : 32 * q + 4 * PASSES, :].bitcast(I32),
-                    in_=x_scales[:, 4 * q : 4 * q + 4, :].bitcast(I32),
-                )
-            for o in range(PASSES):
-                for q in range(3, 4):
-                    nc.sync.dma_start(
-                        out=scale_win[32 * q + 4 * o : 32 * q + 4 * o + 4, :].bitcast(I32),
-                        in_=x_scales[o, 4 * q : 4 * q + 4, :].bitcast(I32),
-                    )
+        def load_pair(u):
+            (o, d), (o_next, d_next) = PIECES[u], PIECES[u + 1]
+            if o_next != o:
+                rows = w[d].rearrange("(o p t) m -> p o (t m)", p=P, t=PACK)
+            else:
+                rows = w[d : d_next + 1, o * K_PASS : (o + 1) * K_PASS, :].rearrange("d (p t) m -> p d (t m)", t=PACK)
+            nc.sync.dma_start(out=w_raw[:, u : u + 2, :], in_=rows)
 
         def load_words(o):
-            nc.sync.dma_start(out=word_win[o][:], in_=x_words[o].rearrange("p c r -> p (c r)").bitcast(I32))
+            nc.sync.dma_start(out=word_win[o][:], in_=x_words[o].rearrange("p c t -> p (c t)").bitcast(I32))
 
-        def load_w(u0, u1):
-            o, d = UNIT[u0]
-            if UNIT[u1 - 1][1] == d and u1 - u0 == PASSES:
-                rows = w[d].rearrange("(o p j) m -> p o (j m)", p=P, j=PACK)
-            else:
-                rows = w[d : d + u1 - u0, o * K_PASS : (o + 1) * K_PASS, :].rearrange("d (p j) m -> p d (j m)", j=PACK)
-            nc.sync.dma_start(out=w_raw[:, u0:u1, :], in_=rows)
-
-        def cast_w(u):
-            nc.scalar.copy(
-                out=w_bf[:, u * K_PASS : (u + 1) * K_PASS].rearrange("p (c i t) -> p c t i", i=4, t=PACK),
-                in_=w_raw[:, u, :].rearrange("p (t c i) -> p c t i", i=4, t=PACK),
+        def load_scale_rows(q, o0, o1):
+            p0 = QUADRANT * q
+            nc.sync.dma_start(
+                out=scale_win[p0 + SCALE_ROWS * o0 : p0 + SCALE_ROWS * o1, :].bitcast(I32),
+                in_=x_scales[o0:o1, SCALE_ROWS * q : SCALE_ROWS * (q + 1), :].bitcast(I32),
             )
 
-        def quantize_w(u0, u1):
+        def quantize(u0, u1):
             nc.vector.quantize_mx(
                 out=w_codes[:, u0 * M : u1 * M].bitcast(FP8X4),
                 scales=w_scale[:, u0 * M : u1 * M],
                 in_=w_bf[:, u0 * K_PASS : u1 * K_PASS],
             )
 
-        def gather(dst, window, e0, e1):
-            nc.vector.tensor_copy(dst[:, e0:e1], window.indirect(offsets[:, e0 // 16 : e1 // 16]))
+        def gather(dst, window, cut):
+            for e0, e1 in ((0, cut), (cut, S)):
+                nc.vector.tensor_copy(dst[:, e0:e1], window.indirect(offsets[:, e0 // LIST_ROWS : e1 // LIST_ROWS]))
 
-        for kind, i, j in DMA_ORDER:
-            if kind == "x":
-                load_words(i)
-            elif kind == "w":
-                load_w(i, j)
-            elif kind == "s":
-                load_scales()
-            else:
-                nc.sync.dma_start(out=bias[:], in_=b)
-        for u in range(UNITS):
-            cast_w(u)
-        for kind, i, j in VEC_ORDER:
-            if kind == "x0":
-                gather(x_codes[0], word_win[0][:].bitcast(U32), i, j)
-            elif kind == "x1":
-                gather(x_codes[1], word_win[1][:].bitcast(U32), i, j)
-            elif kind == "s":
-                gather(x_scale, scale_win[:], i, j)
-            else:
-                quantize_w(i, j)
+        nc.vector.memset(scale_win[:].bitcast(I32), 0)
 
-        for n, u in enumerate(MM_ORDER):
-            o, d = UNIT[u]
-            for h in range(PARTS):
-                cols = slice(d * V + h * PART, d * V + (h + 1) * PART)
+        split, half_row = n_early - 1, K_PASS // 2
+        nc.sync.dma_start(out=w_raw[:, split, :half_row], in_=piece_rows(split)[:, :half_row])
+        nc.sync.dma_start(offsets[:], offs)
+        last_quadrant = P // QUADRANT - 1
+        for q in range(last_quadrant):
+            load_scale_rows(q, 0, PASSES)
+        for o in range(PASSES):
+            load_scale_rows(last_quadrant, o, o + 1)
+        load_words(0)
+        for u in range(0, split, 2):
+            load_pair(u)
+        nc.sync.dma_start(out=w_raw[:, split, half_row:], in_=piece_rows(split)[:, half_row:])
+        load_words(1)
+        for u in range(n_early, n_pieces):
+            nc.sync.dma_start(out=w_raw[:, u, :], in_=piece_rows(u))
+        nc.sync.dma_start(out=bias[:], in_=b)
+
+        for u in range(n_pieces):
+            nc.scalar.copy(
+                out=w_bf[:, u * K_PASS : (u + 1) * K_PASS].rearrange("p (c i t) -> p c t i", i=LINE, t=PACK),
+                in_=w_raw[:, u, :].rearrange("p (t c i) -> p c t i", i=LINE, t=PACK),
+            )
+
+        gather(x_scale, scale_win[:], FIRST_CUT)
+        gather(x_codes[0], word_win[0][:].bitcast(U32), FIRST_CUT)
+        quantize(0, 4)
+        quantize(4, 6)
+        quantize(6, n_early)
+        gather(x_codes[1], word_win[1][:].bitcast(U32), FIRST_CUT_PASS_1)
+        for u in range(n_early, n_pieces, 2):
+            quantize(u, min(u + 2, n_pieces))
+
+        order = [1, 0] + list(range(2, n_pieces))
+        for u in order:
+            o, d = PIECES[u]
+            for h in range(2):
+                cols = slice(d * V + h * HALF, d * V + (h + 1) * HALF)
                 nc.tensor.matmul_mx(
                     out=acc[h][:],
                     lhsT=w_codes[:, u * M : (u + 1) * M].bitcast(FP8X4),
                     lhsT_scale=w_scale[:, u * M : (u + 1) * M],
                     rhs=x_codes[o][:, cols].bitcast(FP8X4),
-                    rhs_scale=x_scale[4 * o :, cols],
-                    start=(n == 0),
-                    stop=(n == UNITS - 1),
+                    rhs_scale=x_scale[SCALE_ROWS * o :, cols],
+                    start=(u == order[0]),
+                    stop=(u == order[-1]),
                 )
-        result = [keep.tile([M, PART], F32, name="result%d" % h) for h in range(PARTS)]
+
+        result = [keep.tile([M, HALF], F32, name="result%d" % h) for h in range(2)]
         nc.scalar.activation(result[0][:], acc[0][:], mybir.ActivationFunctionType.Identity, bias=bias[:])
-        nc.scalar.dma_start(out=out[:, :PART], in_=result[0][:])
+        nc.scalar.dma_start(out=out[:, :HALF], in_=result[0][:])
         nc.vector.tensor_scalar_add(result[1][:], acc[1][:], bias[:])
-        nc.sync.dma_start(out=out[:, PART:], in_=result[1][:])
+        nc.sync.dma_start(out=out[:, HALF:], in_=result[1][:])

@@ -87,11 +87,10 @@ def tile_picked_deform_lin_bias_def_p_kernel(tc, x_words, x_scales, w, b, offs, 
         split, half_row = n_early - 1, K_PASS // 2
         nc.sync.dma_start(out=w_raw[:, split, :half_row], in_=piece_rows(split)[:, :half_row])
         nc.sync.dma_start(offsets[:], offs)
-        last_quadrant = P // QUADRANT - 1
-        for q in range(last_quadrant):
+        for q in (2, 3, 0):
             load_scale_rows(q, 0, PASSES)
         for o in range(PASSES):
-            load_scale_rows(last_quadrant, o, o + 1)
+            load_scale_rows(1, o, o + 1)
         load_words(0)
         for u in range(0, split, 2):
             load_pair(u)

@@ -15,10 +15,10 @@ LINE = 4
 HALF = V // 2
 FLOPS = 2 * S * K * M
 
-EARLY = [(0, 0), (1, 0)] + [(0, d) for d in range(1, TAPS - 1)]
+EARLY = [(0, 1), (0, 0), (1, 0)] + [(0, d) for d in range(2, TAPS - 1)]
 LATE = [(1, d) for d in range(1, TAPS - 1)] + [(0, TAPS - 1), (1, TAPS - 1)]
 PIECES = EARLY + LATE
-FIRST_CUT = 4 * V
+WIDE = 2 * S
 FIRST_CUT_PASS_1 = 3 * V
 
 F32 = mybir.dt.float32
@@ -38,8 +38,8 @@ def tile_picked_deform_lin_bias_def_p_kernel(tc, x_words, x_scales, w, b, offs, 
         psum = ctx.enter_context(tc.psum_pool(name="psum", bufs=1))
 
         offsets = keep.tile([P, S // LIST_ROWS], U16, name="offsets")
-        word_win = [keep.tile([P, T], I32, name="word_win%d" % o, align_bytes=64) for o in range(PASSES)]
-        scale_win = keep.tile([P, T], U8, name="scale_win", align_bytes=64)
+        word_win = [keep.tile([P, (WIDE, T)[o]], I32, name="word_win%d" % o, align_bytes=64) for o in range(PASSES)]
+        scale_win = keep.tile([P, WIDE], U8, name="scale_win", align_bytes=64)
         x_codes = [keep.tile([P, S], U32, name="x_codes%d" % o, align_bytes=64) for o in range(PASSES)]
         x_scale = keep.tile([P, S], U8, name="x_scale", align_bytes=64)
         bias = keep.tile([P, 1], F32, name="bias")
@@ -62,12 +62,12 @@ def tile_picked_deform_lin_bias_def_p_kernel(tc, x_words, x_scales, w, b, offs, 
             nc.sync.dma_start(out=w_raw[:, u : u + 2, :], in_=rows)
 
         def load_words(o):
-            nc.sync.dma_start(out=word_win[o][:], in_=x_words[o].rearrange("p c t -> p (c t)").bitcast(I32))
+            nc.sync.dma_start(out=word_win[o][:, :T], in_=x_words[o].rearrange("p c t -> p (c t)").bitcast(I32))
 
         def load_scale_rows(q, o0, o1):
             p0 = QUADRANT * q
             nc.sync.dma_start(
-                out=scale_win[p0 + SCALE_ROWS * o0 : p0 + SCALE_ROWS * o1, :].bitcast(I32),
+                out=scale_win[p0 + SCALE_ROWS * o0 : p0 + SCALE_ROWS * o1, :T].bitcast(I32),
                 in_=x_scales[o0:o1, SCALE_ROWS * q : SCALE_ROWS * (q + 1), :].bitcast(I32),
             )
 
@@ -82,19 +82,19 @@ def tile_picked_deform_lin_bias_def_p_kernel(tc, x_words, x_scales, w, b, offs, 
             for e0, e1 in ((0, cut), (cut, S)):
                 nc.vector.tensor_copy(dst[:, e0:e1], window.indirect(offsets[:, e0 // LIST_ROWS : e1 // LIST_ROWS]))
 
-        nc.vector.memset(scale_win[:].bitcast(I32), 0)
+        nc.vector.memset(scale_win[:, :T].bitcast(I32), 0)
+        nc.vector.memset(scale_win[:, T:].bitcast(I32), 0)
+        nc.vector.memset(word_win[0][:, T:], 0)
 
-        split, half_row = n_early - 1, K_PASS // 2
-        nc.sync.dma_start(out=w_raw[:, split, :half_row], in_=piece_rows(split)[:, :half_row])
+        nc.sync.dma_start(out=w_raw[:, 0, :], in_=piece_rows(0))
         nc.sync.dma_start(offsets[:], offs)
         for q in (2, 3, 0):
             load_scale_rows(q, 0, PASSES)
         for o in range(PASSES):
             load_scale_rows(1, o, o + 1)
         load_words(0)
-        for u in range(0, split, 2):
+        for u in range(1, n_early, 2):
             load_pair(u)
-        nc.sync.dma_start(out=w_raw[:, split, half_row:], in_=piece_rows(split)[:, half_row:])
         load_words(1)
         for u in range(n_early, n_pieces):
             nc.sync.dma_start(out=w_raw[:, u, :], in_=piece_rows(u))
@@ -106,16 +106,16 @@ def tile_picked_deform_lin_bias_def_p_kernel(tc, x_words, x_scales, w, b, offs, 
                 in_=w_raw[:, u, :].rearrange("p (t c i) -> p c t i", i=LINE, t=PACK),
             )
 
-        gather(x_scale, scale_win[:], FIRST_CUT)
-        gather(x_codes[0], word_win[0][:].bitcast(U32), FIRST_CUT)
-        quantize(0, 4)
-        quantize(4, 6)
-        quantize(6, n_early)
+        quantize(0, 1)
+        nc.vector.tensor_copy(x_scale[:], scale_win[:].indirect(offsets[:]))
+        nc.vector.tensor_copy(x_codes[0][:], word_win[0][:].bitcast(U32).indirect(offsets[:]))
+        quantize(1, 5)
+        quantize(5, n_early)
         gather(x_codes[1], word_win[1][:].bitcast(U32), FIRST_CUT_PASS_1)
         for u in range(n_early, n_pieces, 2):
             quantize(u, min(u + 2, n_pieces))
 
-        order = [1, 0] + list(range(2, n_pieces))
+        order = [2, 0, 1] + list(range(3, n_pieces))
         for u in order:
             o, d = PIECES[u]
             for h in range(2):

@@ -101,7 +101,8 @@ def tile_picked_deform_lin_bias_def_p_kernel(tc, x_words, x_scales, w, b, offs, 
         nc.sync.dma_start(out=bias[:], in_=b)
 
         for u in range(n_pieces):
-            nc.scalar.copy(
+            cast = nc.vector.tensor_copy if u == 0 else nc.scalar.copy
+            cast(
                 out=w_bf[:, u * K_PASS : (u + 1) * K_PASS].rearrange("p (c i t) -> p c t i", i=LINE, t=PACK),
                 in_=w_raw[:, u, :].rearrange("p (t c i) -> p c t i", i=LINE, t=PACK),
             )
@@ -112,8 +113,8 @@ def tile_picked_deform_lin_bias_def_p_kernel(tc, x_words, x_scales, w, b, offs, 
         quantize(1, 5)
         quantize(5, n_early)
         gather(x_codes[1], word_win[1][:].bitcast(U32), FIRST_CUT_PASS_1)
-        for u in range(n_early, n_pieces, 2):
-            quantize(u, min(u + 2, n_pieces))
+        for u in range(n_early, n_pieces):
+            quantize(u, u + 1)
 
         order = [2, 0, 1] + list(range(3, n_pieces))
         for u in order:
@@ -131,7 +132,7 @@ def tile_picked_deform_lin_bias_def_p_kernel(tc, x_words, x_scales, w, b, offs, 
                 )
 
         result = [keep.tile([M, HALF], F32, name="result%d" % h) for h in range(2)]
-        nc.scalar.activation(result[0][:], acc[0][:], mybir.ActivationFunctionType.Identity, bias=bias[:])
-        nc.scalar.dma_start(out=out[:, :HALF], in_=result[0][:])
-        nc.vector.tensor_scalar_add(result[1][:], acc[1][:], bias[:])
-        nc.sync.dma_start(out=out[:, HALF:], in_=result[1][:])
+        nc.vector.tensor_scalar_add(result[0][:], acc[0][:], bias[:])
+        nc.sync.dma_start(out=out[:, :HALF], in_=result[0][:])
+        nc.scalar.activation(result[1][:], acc[1][:], mybir.ActivationFunctionType.Identity, bias=bias[:])
+        nc.scalar.dma_start(out=out[:, HALF:], in_=result[1][:])

@@ -15,8 +15,8 @@ LINE = 4
 HALF = V // 2
 FLOPS = 2 * S * K * M
 
-EARLY = [(0, 1), (0, 0), (1, 0)] + [(0, d) for d in range(2, TAPS - 1)]
-LATE = [(1, d) for d in range(1, TAPS - 1)] + [(0, TAPS - 1), (1, TAPS - 1)]
+EARLY = [(0, 1), (0, 0), (1, 0)] + [(0, d) for d in range(2, TAPS - 2)]
+LATE = [(0, TAPS - 2)] + [(1, d) for d in range(1, TAPS - 1)] + [(0, TAPS - 1), (1, TAPS - 1)]
 PIECES = EARLY + LATE
 WIDE = 2 * S
 FIRST_CUT_PASS_1 = 3 * V
@@ -93,8 +93,9 @@ def tile_picked_deform_lin_bias_def_p_kernel(tc, x_words, x_scales, w, b, offs, 
         for o in range(PASSES):
             load_scale_rows(1, o, o + 1)
         load_words(0)
-        for u in range(1, n_early, 2):
+        for u in range(1, n_early - 1, 2):
             load_pair(u)
+        nc.sync.dma_start(out=w_raw[:, n_early - 1, :], in_=piece_rows(n_early - 1))
         load_words(1)
         for u in range(n_early, n_pieces):
             nc.sync.dma_start(out=w_raw[:, u, :], in_=piece_rows(u))

@@ -86,12 +86,12 @@ def tile_picked_deform_lin_bias_def_p_kernel(tc, x_words, x_scales, w, b, offs, 
         nc.vector.memset(scale_win[:, T:].bitcast(I32), 0)
         nc.vector.memset(word_win[0][:, T:], 0)
 
-        nc.sync.dma_start(out=w_raw[:, 0, :], in_=piece_rows(0))
         nc.sync.dma_start(offsets[:], offs)
-        for q in (2, 3, 0):
+        nc.sync.dma_start(out=w_raw[:, 0, :], in_=piece_rows(0))
+        for q in (2, 0):
             load_scale_rows(q, 0, PASSES)
-        for o in range(PASSES):
-            load_scale_rows(1, o, o + 1)
+        for q, o in ((3, 0), (1, 1), (3, 1), (1, 0)):
+            load_scale_rows(q, o, o + 1)
         load_words(0)
         for u in range(1, n_early - 1, 2):
             load_pair(u)

@@ -9,17 +9,20 @@ PACK = 4
 K_PASS = P * PACK
 PASSES = K // K_PASS
 QUADRANT = 32
+QUADRANTS = P // QUADRANT
 SCALE_ROWS = 4
 LIST_ROWS = 16
 LINE = 4
 HALF = V // 2
 FLOPS = 2 * S * K * M
 
-EARLY = [(0, 1), (0, 0), (1, 0)] + [(0, d) for d in range(2, TAPS - 2)]
-LATE = [(0, TAPS - 2)] + [(1, d) for d in range(1, TAPS - 1)] + [(0, TAPS - 1), (1, TAPS - 1)]
-PIECES = EARLY + LATE
+EARLY_TAPS = 3
+EARLY = [(0, 0), (1, 0)] + [(0, d) for d in range(1, 1 + EARLY_TAPS)]
+MIDDLE = [(0, d) for d in range(1 + EARLY_TAPS, TAPS - 1)]
+LATE = [(1, d) for d in range(1, TAPS - 1)] + [(0, TAPS - 1), (1, TAPS - 1)]
+PIECES = EARLY + MIDDLE + LATE
 WIDE = 2 * S
-FIRST_CUT_PASS_1 = 3 * V
+CUT = [4 * V, 3 * V]
 
 F32 = mybir.dt.float32
 BF16 = mybir.dt.bfloat16
@@ -32,43 +35,40 @@ FP8X4 = mybir.dt.float8_e4m3fn_x4
 
 def tile_picked_deform_lin_bias_def_p_kernel(tc, x_words, x_scales, w, b, offs, out):
     nc = tc.nc
-    n_early, n_pieces = len(EARLY), len(PIECES)
+    n_early, n_middle, n_pieces = len(EARLY), len(MIDDLE), len(PIECES)
+    first_late, last = n_early + n_middle, n_pieces - 1
     with ExitStack() as ctx:
         keep = ctx.enter_context(tc.tile_pool(name="keep", bufs=1))
         psum = ctx.enter_context(tc.psum_pool(name="psum", bufs=1))
 
         offsets = keep.tile([P, S // LIST_ROWS], U16, name="offsets")
-        word_win = [keep.tile([P, (WIDE, T)[o]], I32, name="word_win%d" % o, align_bytes=64) for o in range(PASSES)]
+        word_win = [keep.tile([P, T], I32, name="word_win%d" % o, align_bytes=64) for o in range(PASSES)]
         scale_win = keep.tile([P, WIDE], U8, name="scale_win", align_bytes=64)
-        x_codes = [keep.tile([P, S], U32, name="x_codes%d" % o, align_bytes=64) for o in range(PASSES)]
+        x_codes_0 = keep.tile([P, S], U32, name="x_codes_0", align_bytes=64)
+        x_codes_1 = keep.tile([P, CUT[1]], U32, name="x_codes_1", align_bytes=64)
+        x_scale_dense = keep.tile([P, S], U8, name="x_scale_dense", align_bytes=64)
         x_scale = keep.tile([P, S], U8, name="x_scale", align_bytes=64)
-        bias = keep.tile([P, 1], F32, name="bias")
-        w_raw = keep.tile([P, n_pieces, K_PASS], F32, name="w_raw", align_bytes=64)
         w_bf = keep.tile([P, n_pieces * K_PASS], BF16, name="w_bf", align_bytes=64)
         w_codes = keep.tile([P, n_pieces * M], U32, name="w_codes", align_bytes=64)
         w_scale = keep.tile([P, n_pieces * M], U8, name="w_scale", align_bytes=64)
         acc = [psum.tile([M, HALF], F32, name="acc%d" % h) for h in range(2)]
 
-        def piece_rows(u):
-            o, d = PIECES[u]
-            return w[d, o * K_PASS : (o + 1) * K_PASS, :].rearrange("(p t) m -> p (t m)", t=PACK)
+        def raw_tile(name, tag, pieces):
+            return keep.tile([P, pieces, K_PASS], F32, name=name, tag=tag, align_bytes=64)
 
-        def load_pair(u):
-            (o, d), (o_next, d_next) = PIECES[u], PIECES[u + 1]
-            if o_next != o:
-                rows = w[d].rearrange("(o p t) m -> p o (t m)", p=P, t=PACK)
-            else:
-                rows = w[d : d_next + 1, o * K_PASS : (o + 1) * K_PASS, :].rearrange("d (p t) m -> p d (t m)", t=PACK)
-            nc.sync.dma_start(out=w_raw[:, u : u + 2, :], in_=rows)
+        def load_piece(u, raw):
+            o, d = PIECES[u]
+            rows = w[d, o * K_PASS : (o + 1) * K_PASS, :]
+            nc.sync.dma_start(out=raw, in_=rows.rearrange("(p t) m -> p (t m)", t=PACK))
 
         def load_words(o):
-            nc.sync.dma_start(out=word_win[o][:, :T], in_=x_words[o].rearrange("p c t -> p (c t)").bitcast(I32))
+            nc.sync.dma_start(out=word_win[o][:], in_=x_words[o].rearrange("p c t -> p (c t)").bitcast(I32))
 
-        def load_scale_rows(q, o0, o1):
-            p0 = QUADRANT * q
-            nc.sync.dma_start(
-                out=scale_win[p0 + SCALE_ROWS * o0 : p0 + SCALE_ROWS * o1, :T].bitcast(I32),
-                in_=x_scales[o0:o1, SCALE_ROWS * q : SCALE_ROWS * (q + 1), :].bitcast(I32),
+        def cast(copy, u, raw, m0, m1):
+            lines = slice(m0 // LINE, m1 // LINE)
+            copy(
+                out=w_bf[:, u * K_PASS : (u + 1) * K_PASS].rearrange("p (c i t) -> p c t i", i=LINE, t=PACK)[:, lines],
+                in_=raw.rearrange("p (t c i) -> p c t i", i=LINE, t=PACK)[:, lines],
             )
 
         def quantize(u0, u1):
@@ -78,56 +78,85 @@ def tile_picked_deform_lin_bias_def_p_kernel(tc, x_words, x_scales, w, b, offs, 
                 in_=w_bf[:, u0 * K_PASS : u1 * K_PASS],
             )
 
-        def gather(dst, window, cut):
-            for e0, e1 in ((0, cut), (cut, S)):
-                nc.vector.tensor_copy(dst[:, e0:e1], window.indirect(offsets[:, e0 // LIST_ROWS : e1 // LIST_ROWS]))
+        def gather(dst, window, e0, e1):
+            nc.vector.tensor_copy(dst, window.indirect(offsets[:, e0 // LIST_ROWS : e1 // LIST_ROWS]))
 
-        nc.vector.memset(scale_win[:, :T].bitcast(I32), 0)
+        nc.vector.memset(scale_win[QUADRANT : 2 * QUADRANT, :T].bitcast(I32), 0)
+        nc.vector.memset(scale_win[2 * QUADRANT :, :T].bitcast(I32), 0)
         nc.vector.memset(scale_win[:, T:].bitcast(I32), 0)
-        nc.vector.memset(word_win[0][:, T:], 0)
+        nc.vector.memset(x_scale[:].bitcast(I32), 0)
 
         nc.sync.dma_start(offsets[:], offs)
-        nc.sync.dma_start(out=w_raw[:, 0, :], in_=piece_rows(0))
-        for q in (2, 0):
-            load_scale_rows(q, 0, PASSES)
-        for q, o in ((3, 0), (1, 1), (3, 1), (1, 0)):
-            load_scale_rows(q, o, o + 1)
+        rows_a_pass = QUADRANTS * SCALE_ROWS
+        for o in range(PASSES):
+            nc.sync.dma_start(
+                out=scale_win[rows_a_pass * o : rows_a_pass * (o + 1), :T].bitcast(I32),
+                in_=x_scales[o].bitcast(I32).rearrange("(q r) c -> r q c", r=SCALE_ROWS),
+            )
         load_words(0)
-        for u in range(1, n_early - 1, 2):
-            load_pair(u)
-        nc.sync.dma_start(out=w_raw[:, n_early - 1, :], in_=piece_rows(n_early - 1))
+        raw_tap_0 = raw_tile("raw_tap_0", "tap_0", PASSES)
+        nc.sync.dma_start(out=raw_tap_0[:], in_=w[0].rearrange("(o p t) m -> p o (t m)", p=P, t=PACK))
+        raw_early = raw_tile("raw_early", "early", EARLY_TAPS)
+        nc.sync.dma_start(
+            out=raw_early[:], in_=w[1 : 1 + EARLY_TAPS, :K_PASS, :].rearrange("d (p t) m -> p d (t m)", t=PACK)
+        )
         load_words(1)
-        for u in range(n_early, n_pieces):
-            nc.sync.dma_start(out=w_raw[:, u, :], in_=piece_rows(u))
+        raw_middle = raw_tile("raw_middle", "middle", n_middle)
+        for j in range(n_middle):
+            load_piece(n_early + j, raw_middle[:, j, :])
+        raws = [raw_tap_0[:, j, :] for j in range(PASSES)] + [raw_early[:, j, :] for j in range(EARLY_TAPS)]
+        raws = raws + [raw_middle[:, j, :] for j in range(n_middle)]
+        for u in range(first_late):
+            cast(nc.scalar.copy, u, raws[u], 0, M)
+
+        gather(x_scale_dense[:], scale_win[:], 0, S)
+        for q in (0, 2, 1, 3):
+            nc.sync.dma_start(
+                out=x_scale[QUADRANT * q : QUADRANT * q + PASSES * SCALE_ROWS, :].bitcast(I32),
+                in_=x_scale_dense[q:QUADRANT:QUADRANTS, :].bitcast(I32),
+            )
+        u = first_late
+        for tag, pieces in (("tap_0", PASSES), ("early", len(LATE) - PASSES)):
+            raw_late = raw_tile("raw_late_" + tag, tag, pieces)
+            for j in range(pieces):
+                load_piece(u, raw_late[:, j, :])
+                cast(nc.scalar.copy, u, raw_late[:, j, :], 0, M if u < last else M // 2)
+                u = u + 1
+        bias = keep.tile([P, 1], F32, name="bias", tag="tap_0", align_bytes=64)
         nc.sync.dma_start(out=bias[:], in_=b)
 
-        for u in range(n_pieces):
-            cast = nc.vector.tensor_copy if u == 0 else nc.scalar.copy
-            cast(
-                out=w_bf[:, u * K_PASS : (u + 1) * K_PASS].rearrange("p (c i t) -> p c t i", i=LINE, t=PACK),
-                in_=w_raw[:, u, :].rearrange("p (t c i) -> p c t i", i=LINE, t=PACK),
-            )
-
-        quantize(0, 1)
-        nc.vector.tensor_copy(x_scale[:], scale_win[:].indirect(offsets[:]))
-        nc.vector.tensor_copy(x_codes[0][:], word_win[0][:].bitcast(U32).indirect(offsets[:]))
-        quantize(1, 5)
-        quantize(5, n_early)
-        gather(x_codes[1], word_win[1][:].bitcast(U32), FIRST_CUT_PASS_1)
-        for u in range(n_early, n_pieces):
+        gather(x_codes_0[:, : CUT[0]], word_win[0][:].bitcast(U32), 0, CUT[0])
+        gather(x_codes_0[:, CUT[0] :], word_win[0][:].bitcast(U32), CUT[0], S)
+        quantize(0, n_early - 1)
+        quantize(n_early - 1, n_early)
+        gather(x_codes_1[:], word_win[1][:].bitcast(U32), 0, CUT[1])
+        quantize(n_early, first_late)
+        x_codes_1_rest = keep.tile([P, S - CUT[1]], U32, name="x_codes_1_rest", tag="middle", align_bytes=64)
+        gather(x_codes_1_rest[:], word_win[1][:].bitcast(U32), CUT[1], S)
+        for u in range(first_late, last - 1):
             quantize(u, u + 1)
+        cast(nc.vector.tensor_copy, last, raw_late[:, len(LATE) - PASSES - 1, :], M // 2, M)
+        quantize(last - 1, last)
+        quantize(last, n_pieces)
 
-        order = [2, 0, 1] + list(range(3, n_pieces))
+        def picked(o, e0):
+            if o == 0:
+                return x_codes_0[:, e0 : e0 + HALF]
+            if e0 < CUT[1]:
+                return x_codes_1[:, e0 : e0 + HALF]
+            return x_codes_1_rest[:, e0 - CUT[1] : e0 - CUT[1] + HALF]
+
+        order = [1, 0] + list(range(2, n_pieces))
         for u in order:
             o, d = PIECES[u]
             for h in range(2):
-                cols = slice(d * V + h * HALF, d * V + (h + 1) * HALF)
+                e0 = d * V + h * HALF
                 nc.tensor.matmul_mx(
                     out=acc[h][:],
                     lhsT=w_codes[:, u * M : (u + 1) * M].bitcast(FP8X4),
                     lhsT_scale=w_scale[:, u * M : (u + 1) * M],
-                    rhs=x_codes[o][:, cols].bitcast(FP8X4),
-                    rhs_scale=x_scale[SCALE_ROWS * o :, cols],
+                    rhs=picked(o, e0).bitcast(FP8X4),
+                    rhs_scale=x_scale[SCALE_ROWS * o :, e0 : e0 + HALF],
                     start=(u == order[0]),
                     stop=(u == order[-1]),
                 )

@@ -16,13 +16,15 @@ LINE = 4
 HALF = V // 2
 FLOPS = 2 * S * K * M
 
-EARLY_TAPS = 3
-EARLY = [(0, 0), (1, 0)] + [(0, d) for d in range(1, 1 + EARLY_TAPS)]
-MIDDLE = [(0, d) for d in range(1 + EARLY_TAPS, TAPS - 1)]
-LATE = [(1, d) for d in range(1, TAPS - 1)] + [(0, TAPS - 1), (1, TAPS - 1)]
+MIDDLE_TAPS = 4
+EARLY = [(0, 0), (1, 0)]
+MIDDLE = [(0, d) for d in range(1, 1 + MIDDLE_TAPS)]
+LATE = [(0, d) for d in range(1 + MIDDLE_TAPS, TAPS)] + [(1, d) for d in range(1, TAPS)]
 PIECES = EARLY + MIDDLE + LATE
 WIDE = 2 * S
 CUT = [4 * V, 3 * V]
+CUT_1 = [0, 4 * V, 6 * V, S]
+SLOT = K_PASS * 4
 
 F32 = mybir.dt.float32
 BF16 = mybir.dt.bfloat16
@@ -35,17 +37,18 @@ FP8X4 = mybir.dt.float8_e4m3fn_x4
 
 def tile_picked_deform_lin_bias_def_p_kernel(tc, x_words, x_scales, w, b, offs, out):
     nc = tc.nc
-    n_early, n_middle, n_pieces = len(EARLY), len(MIDDLE), len(PIECES)
-    first_late, last = n_early + n_middle, n_pieces - 1
+    n_early, n_pieces = len(EARLY), len(PIECES)
+    first_late, last = n_early + len(MIDDLE), n_pieces - 1
     with ExitStack() as ctx:
         keep = ctx.enter_context(tc.tile_pool(name="keep", bufs=1))
+        room = ctx.enter_context(tc.tile_pool(name="room", bufs=1))
         psum = ctx.enter_context(tc.psum_pool(name="psum", bufs=1))
 
         offsets = keep.tile([P, S // LIST_ROWS], U16, name="offsets")
         word_win = [keep.tile([P, T], I32, name="word_win%d" % o, align_bytes=64) for o in range(PASSES)]
         scale_win = keep.tile([P, WIDE], U8, name="scale_win", align_bytes=64)
         x_codes_0 = keep.tile([P, S], U32, name="x_codes_0", align_bytes=64)
-        x_codes_1 = keep.tile([P, CUT[1]], U32, name="x_codes_1", align_bytes=64)
+        x_codes_1 = [keep.tile([P, CUT_1[1]], U32, name="x_codes_1_0", align_bytes=64)]
         x_scale_dense = keep.tile([P, S], U8, name="x_scale_dense", align_bytes=64)
         x_scale = keep.tile([P, S], U8, name="x_scale", align_bytes=64)
         w_bf = keep.tile([P, n_pieces * K_PASS], BF16, name="w_bf", align_bytes=64)
@@ -53,8 +56,8 @@ def tile_picked_deform_lin_bias_def_p_kernel(tc, x_words, x_scales, w, b, offs, 
         w_scale = keep.tile([P, n_pieces * M], U8, name="w_scale", align_bytes=64)
         acc = [psum.tile([M, HALF], F32, name="acc%d" % h) for h in range(2)]
 
-        def raw_tile(name, tag, pieces):
-            return keep.tile([P, pieces, K_PASS], F32, name=name, tag=tag, align_bytes=64)
+        def raw_tile(name, slot, pieces):
+            return room.tile([P, pieces, K_PASS], F32, name=name, offset=slot * SLOT, align_bytes=64)
 
         def load_piece(u, raw):
             o, d = PIECES[u]
@@ -94,20 +97,18 @@ def tile_picked_deform_lin_bias_def_p_kernel(tc, x_words, x_scales, w, b, offs, 
                 in_=x_scales[o].bitcast(I32).rearrange("(q r) c -> r q c", r=SCALE_ROWS),
             )
         load_words(0)
-        raw_tap_0 = raw_tile("raw_tap_0", "tap_0", PASSES)
+        raw_tap_0 = raw_tile("raw_tap_0", 0, PASSES)
         nc.sync.dma_start(out=raw_tap_0[:], in_=w[0].rearrange("(o p t) m -> p o (t m)", p=P, t=PACK))
-        raw_early = raw_tile("raw_early", "early", EARLY_TAPS)
-        nc.sync.dma_start(
-            out=raw_early[:], in_=w[1 : 1 + EARLY_TAPS, :K_PASS, :].rearrange("d (p t) m -> p d (t m)", t=PACK)
-        )
         load_words(1)
-        raw_middle = raw_tile("raw_middle", "middle", n_middle)
-        for j in range(n_middle):
-            load_piece(n_early + j, raw_middle[:, j, :])
-        raws = [raw_tap_0[:, j, :] for j in range(PASSES)] + [raw_early[:, j, :] for j in range(EARLY_TAPS)]
-        raws = raws + [raw_middle[:, j, :] for j in range(n_middle)]
-        for u in range(first_late):
-            cast(nc.scalar.copy, u, raws[u], 0, M)
+        for u in range(n_early):
+            cast(nc.scalar.copy, u, raw_tap_0[:, u, :], 0, M)
+        for u in range(n_early, first_late, 2):
+            raw_middle = raw_tile("raw_middle%d" % u, first_late - u, 2)
+            o, d = PIECES[u]
+            rows = w[d : d + 2, o * K_PASS : (o + 1) * K_PASS, :]
+            nc.sync.dma_start(out=raw_middle[:], in_=rows.rearrange("d (p t) m -> p d (t m)", t=PACK))
+            for j in range(2):
+                cast(nc.scalar.copy, u + j, raw_middle[:, j, :], 0, M)
 
         gather(x_scale_dense[:], scale_win[:], 0, S)
         for q in (0, 2, 1, 3):
@@ -115,36 +116,41 @@ def tile_picked_deform_lin_bias_def_p_kernel(tc, x_words, x_scales, w, b, offs, 
                 out=x_scale[QUADRANT * q : QUADRANT * q + PASSES * SCALE_ROWS, :].bitcast(I32),
                 in_=x_scale_dense[q:QUADRANT:QUADRANTS, :].bitcast(I32),
             )
-        u = first_late
-        for tag, pieces in (("tap_0", PASSES), ("early", len(LATE) - PASSES)):
-            raw_late = raw_tile("raw_late_" + tag, tag, pieces)
-            for j in range(pieces):
-                load_piece(u, raw_late[:, j, :])
-                cast(nc.scalar.copy, u, raw_late[:, j, :], 0, M if u < last else M // 2)
-                u = u + 1
-        bias = keep.tile([P, 1], F32, name="bias", tag="tap_0", align_bytes=64)
+        for j in range(n_early):
+            raw_late = raw_tile("raw_late%d" % j, j, 1)
+            load_piece(first_late + j, raw_late[:, 0, :])
+            cast(nc.scalar.copy, first_late + j, raw_late[:, 0, :], 0, M)
+        raw_late = raw_tile("raw_rest", first_late - n_early, len(LATE) - n_early)
+        for j in range(len(LATE) - n_early):
+            u = first_late + n_early + j
+            load_piece(u, raw_late[:, j, :])
+            cast(nc.scalar.copy, u, raw_late[:, j, :], 0, M if u < last else M // 2)
+        bias = room.tile([P, 1], F32, name="bias", offset=0, align_bytes=64)
         nc.sync.dma_start(out=bias[:], in_=b)
 
         gather(x_codes_0[:, : CUT[0]], word_win[0][:].bitcast(U32), 0, CUT[0])
         gather(x_codes_0[:, CUT[0] :], word_win[0][:].bitcast(U32), CUT[0], S)
-        quantize(0, n_early - 1)
-        quantize(n_early - 1, n_early)
-        gather(x_codes_1[:], word_win[1][:].bitcast(U32), 0, CUT[1])
+        quantize(0, n_early)
+        gather(x_codes_1[0][:], word_win[1][:].bitcast(U32), CUT_1[0], CUT_1[1])
         quantize(n_early, first_late)
-        x_codes_1_rest = keep.tile([P, S - CUT[1]], U32, name="x_codes_1_rest", tag="middle", align_bytes=64)
-        gather(x_codes_1_rest[:], word_win[1][:].bitcast(U32), CUT[1], S)
-        for u in range(first_late, last - 1):
+        for c, slot in ((1, n_early), (2, n_early - 1)):
+            x_codes_1.append(
+                room.tile([P, CUT_1[c + 1] - CUT_1[c]], U32, name="x_codes_1_%d" % c, offset=slot * SLOT, align_bytes=64)
+            )
+            gather(x_codes_1[c][:], word_win[1][:].bitcast(U32), CUT_1[c], CUT_1[c + 1])
+            if c == 1:
+                quantize(first_late, first_late + n_early)
+        for u in range(first_late + n_early, last - 1):
             quantize(u, u + 1)
-        cast(nc.vector.tensor_copy, last, raw_late[:, len(LATE) - PASSES - 1, :], M // 2, M)
+        cast(nc.vector.tensor_copy, last, raw_late[:, len(LATE) - n_early - 1, :], M // 2, M)
         quantize(last - 1, last)
         quantize(last, n_pieces)
 
         def picked(o, e0):
             if o == 0:
                 return x_codes_0[:, e0 : e0 + HALF]
-            if e0 < CUT[1]:
-                return x_codes_1[:, e0 : e0 + HALF]
-            return x_codes_1_rest[:, e0 - CUT[1] : e0 - CUT[1] + HALF]
+            c = sum(e0 >= cut for cut in CUT_1[1:])
+            return x_codes_1[c][:, e0 - CUT_1[c] : e0 - CUT_1[c] + HALF]
 
         order = [1, 0] + list(range(2, n_pieces))
         for u in order:

@@ -14,15 +14,12 @@ SCALE_ROWS = 4
 LIST_ROWS = 16
 LINE = 4
 HALF = V // 2
+ALIGN = 256
 FLOPS = 2 * S * K * M
 
-MIDDLE_TAPS = 4
-EARLY = [(0, 0), (1, 0)]
-MIDDLE = [(0, d) for d in range(1, 1 + MIDDLE_TAPS)]
-LATE = [(0, d) for d in range(1 + MIDDLE_TAPS, TAPS)] + [(1, d) for d in range(1, TAPS)]
-PIECES = EARLY + MIDDLE + LATE
+PIECES = [(0, 0), (1, 0)] + [(o, d) for o in range(PASSES) for d in range(1, TAPS)]
 WIDE = 2 * S
-CUT = [4 * V, 3 * V]
+CUT_0 = [0, 4 * V, S]
 CUT_1 = [0, 4 * V, 6 * V, S]
 SLOT = K_PASS * 4
 
@@ -37,32 +34,40 @@ FP8X4 = mybir.dt.float8_e4m3fn_x4
 
 def tile_picked_deform_lin_bias_def_p_kernel(tc, x_words, x_scales, w, b, offs, out):
     nc = tc.nc
-    n_early, n_pieces = len(EARLY), len(PIECES)
-    first_late, last = n_early + len(MIDDLE), n_pieces - 1
+    n_pieces = len(PIECES)
+    last = n_pieces - 1
     with ExitStack() as ctx:
         keep = ctx.enter_context(tc.tile_pool(name="keep", bufs=1))
         room = ctx.enter_context(tc.tile_pool(name="room", bufs=1))
         psum = ctx.enter_context(tc.psum_pool(name="psum", bufs=1))
 
-        offsets = keep.tile([P, S // LIST_ROWS], U16, name="offsets")
-        word_win = [keep.tile([P, T], I32, name="word_win%d" % o, align_bytes=64) for o in range(PASSES)]
-        scale_win = keep.tile([P, WIDE], U8, name="scale_win", align_bytes=64)
-        x_codes_0 = keep.tile([P, S], U32, name="x_codes_0", align_bytes=64)
-        x_codes_1 = [keep.tile([P, CUT_1[1]], U32, name="x_codes_1_0", align_bytes=64)]
-        x_scale_dense = keep.tile([P, S], U8, name="x_scale_dense", align_bytes=64)
-        x_scale = keep.tile([P, S], U8, name="x_scale", align_bytes=64)
-        w_bf = keep.tile([P, n_pieces * K_PASS], BF16, name="w_bf", align_bytes=64)
-        w_codes = keep.tile([P, n_pieces * M], U32, name="w_codes", align_bytes=64)
-        w_scale = keep.tile([P, n_pieces * M], U8, name="w_scale", align_bytes=64)
+        at_a = 0
+        at_scale = 2 * SLOT - ALIGN
+        at_b = at_scale + WIDE - ALIGN
+        at_tap_0 = at_b + 2 * SLOT
+        at_words_0 = at_tap_0 + 2 * SLOT
+
+        offsets = keep.tile([P, S // LIST_ROWS], U16, name="offsets", align_bytes=ALIGN)
+        scale_win = room.tile([P, WIDE], U8, name="scale_win", offset=at_scale, align_bytes=ALIGN)
+        word_win = [
+            room.tile([P, T], I32, name="word_win0", offset=at_words_0, align_bytes=ALIGN),
+            keep.tile([P, T], I32, name="word_win1", align_bytes=ALIGN),
+        ]
+        x_codes_0 = keep.tile([P, S], U32, name="x_codes_0", align_bytes=ALIGN)
+        x_codes_1 = [keep.tile([P, CUT_1[1]], U32, name="x_codes_1_0", align_bytes=ALIGN)]
+        x_scale_dense = keep.tile([P, S], U8, name="x_scale_dense", align_bytes=ALIGN)
+        x_scale = [keep.tile([P, S], U8, name="x_scale%d" % o, align_bytes=ALIGN) for o in range(PASSES)]
+        w_bf = keep.tile([P, n_pieces * K_PASS], BF16, name="w_bf", align_bytes=ALIGN)
+        w_codes = keep.tile([P, n_pieces * M], U32, name="w_codes", align_bytes=ALIGN)
+        w_scale = keep.tile([P, n_pieces * M], U8, name="w_scale", align_bytes=ALIGN)
         acc = [psum.tile([M, HALF], F32, name="acc%d" % h) for h in range(2)]
 
-        def raw_tile(name, slot, pieces):
-            return room.tile([P, pieces, K_PASS], F32, name=name, offset=slot * SLOT, align_bytes=64)
-
-        def load_piece(u, raw):
+        def load_pieces(u, n, at):
+            raw = room.tile([P, n, K_PASS], F32, name="raw%d" % u, offset=at, align_bytes=ALIGN)
             o, d = PIECES[u]
-            rows = w[d, o * K_PASS : (o + 1) * K_PASS, :]
-            nc.sync.dma_start(out=raw, in_=rows.rearrange("(p t) m -> p (t m)", t=PACK))
+            rows = w[d : d + n, o * K_PASS : (o + 1) * K_PASS, :]
+            nc.sync.dma_start(out=raw[:], in_=rows.rearrange("d (p t) m -> p d (t m)", t=PACK))
+            return raw
 
         def load_words(o):
             nc.sync.dma_start(out=word_win[o][:], in_=x_words[o].rearrange("p c t -> p (c t)").bitcast(I32))
@@ -84,67 +89,73 @@ def tile_picked_deform_lin_bias_def_p_kernel(tc, x_words, x_scales, w, b, offs, 
         def gather(dst, window, e0, e1):
             nc.vector.tensor_copy(dst, window.indirect(offsets[:, e0 // LIST_ROWS : e1 // LIST_ROWS]))
 
-        nc.vector.memset(scale_win[QUADRANT : 2 * QUADRANT, :T].bitcast(I32), 0)
-        nc.vector.memset(scale_win[2 * QUADRANT :, :T].bitcast(I32), 0)
+        first_row = P - QUADRANT
+        rows_a_pass = QUADRANTS * SCALE_ROWS
+
+        def move_scale_rows(o):
+            for r in range(SCALE_ROWS):
+                row = first_row + rows_a_pass * o + r
+                nc.sync.dma_start(
+                    out=x_scale[o][r:P:QUADRANT, :].bitcast(I32),
+                    in_=x_scale_dense[row : first_row + rows_a_pass * (o + 1) : SCALE_ROWS, :].bitcast(I32),
+                )
+
+        nc.vector.memset(scale_win[:first_row, :T].bitcast(I32), 0)
         nc.vector.memset(scale_win[:, T:].bitcast(I32), 0)
-        nc.vector.memset(x_scale[:].bitcast(I32), 0)
+        for o in range(PASSES):
+            nc.vector.memset(x_scale[o][:].bitcast(I32), 0)
 
         nc.sync.dma_start(offsets[:], offs)
-        rows_a_pass = QUADRANTS * SCALE_ROWS
-        for o in range(PASSES):
-            nc.sync.dma_start(
-                out=scale_win[rows_a_pass * o : rows_a_pass * (o + 1), :T].bitcast(I32),
-                in_=x_scales[o].bitcast(I32).rearrange("(q r) c -> r q c", r=SCALE_ROWS),
-            )
+        nc.sync.dma_start(
+            out=scale_win[first_row:, :T].bitcast(I32), in_=x_scales.rearrange("o q c -> (o q) c").bitcast(I32)
+        )
         load_words(0)
-        raw_tap_0 = raw_tile("raw_tap_0", 0, PASSES)
+        raw_tap_0 = room.tile([P, PASSES, K_PASS], F32, name="raw_tap_0", offset=at_tap_0, align_bytes=ALIGN)
         nc.sync.dma_start(out=raw_tap_0[:], in_=w[0].rearrange("(o p t) m -> p o (t m)", p=P, t=PACK))
         load_words(1)
-        for u in range(n_early):
+        for u in range(PASSES):
             cast(nc.scalar.copy, u, raw_tap_0[:, u, :], 0, M)
-        for u in range(n_early, first_late, 2):
-            raw_middle = raw_tile("raw_middle%d" % u, first_late - u, 2)
-            o, d = PIECES[u]
-            rows = w[d : d + 2, o * K_PASS : (o + 1) * K_PASS, :]
-            nc.sync.dma_start(out=raw_middle[:], in_=rows.rearrange("d (p t) m -> p d (t m)", t=PACK))
-            for j in range(2):
-                cast(nc.scalar.copy, u + j, raw_middle[:, j, :], 0, M)
 
         gather(x_scale_dense[:], scale_win[:], 0, S)
-        for q in (0, 2, 1, 3):
-            nc.sync.dma_start(
-                out=x_scale[QUADRANT * q : QUADRANT * q + PASSES * SCALE_ROWS, :].bitcast(I32),
-                in_=x_scale_dense[q:QUADRANT:QUADRANTS, :].bitcast(I32),
-            )
-        for j in range(n_early):
-            raw_late = raw_tile("raw_late%d" % j, j, 1)
-            load_piece(first_late + j, raw_late[:, 0, :])
-            cast(nc.scalar.copy, first_late + j, raw_late[:, 0, :], 0, M)
-        raw_late = raw_tile("raw_rest", first_late - n_early, len(LATE) - n_early)
-        for j in range(len(LATE) - n_early):
-            u = first_late + n_early + j
-            load_piece(u, raw_late[:, j, :])
-            cast(nc.scalar.copy, u, raw_late[:, j, :], 0, M if u < last else M // 2)
-        bias = room.tile([P, 1], F32, name="bias", offset=0, align_bytes=64)
-        nc.sync.dma_start(out=bias[:], in_=b)
+        for c in range(2):
+            gather(x_codes_0[:, CUT_0[c] : CUT_0[c + 1]], word_win[0][:].bitcast(U32), CUT_0[c], CUT_0[c + 1])
 
-        gather(x_codes_0[:, : CUT[0]], word_win[0][:].bitcast(U32), 0, CUT[0])
-        gather(x_codes_0[:, CUT[0] :], word_win[0][:].bitcast(U32), CUT[0], S)
-        quantize(0, n_early)
+        move_scale_rows(0)
+        raw_a = load_pieces(2, 2, at_a)
+        move_scale_rows(1)
+        raw_b = load_pieces(4, 2, at_b)
+        raw_c = load_pieces(6, 2, at_tap_0)
+        raw_d = load_pieces(8, 2, at_words_0)
+        raw_e = load_pieces(10, 2, at_words_0 + 2 * SLOT)
+        for u, raw in ((2, raw_a), (4, raw_b), (6, raw_c), (8, raw_d)):
+            for j in range(2):
+                cast(nc.scalar.copy, u + j, raw[:, j, :], 0, M)
+        cast(nc.scalar.copy, 10, raw_e[:, 0, :], 0, M)
+        raw_f = load_pieces(12, 1, at_a)
+        raw_g = load_pieces(13, 1, at_a + SLOT)
+        bias = room.tile([P, 1], F32, name="bias", offset=at_b + SLOT, align_bytes=ALIGN)
+        nc.sync.dma_start(out=bias[:], in_=b)
+        cast(nc.scalar.copy, 12, raw_f[:, 0, :], 0, M)
+        cast(nc.scalar.copy, 13, raw_g[:, 0, :], 0, M // 2)
+
+        quantize(0, 2)
         gather(x_codes_1[0][:], word_win[1][:].bitcast(U32), CUT_1[0], CUT_1[1])
-        quantize(n_early, first_late)
-        for c, slot in ((1, n_early), (2, n_early - 1)):
+        quantize(2, 4)
+        quantize(4, 6)
+        for c, at in ((1, at_b), (2, at_tap_0)):
             x_codes_1.append(
-                room.tile([P, CUT_1[c + 1] - CUT_1[c]], U32, name="x_codes_1_%d" % c, offset=slot * SLOT, align_bytes=64)
+                room.tile([P, CUT_1[c + 1] - CUT_1[c]], U32, name="x_codes_1_%d" % c, offset=at, align_bytes=ALIGN)
             )
             gather(x_codes_1[c][:], word_win[1][:].bitcast(U32), CUT_1[c], CUT_1[c + 1])
             if c == 1:
-                quantize(first_late, first_late + n_early)
-        for u in range(first_late + n_early, last - 1):
-            quantize(u, u + 1)
-        cast(nc.vector.tensor_copy, last, raw_late[:, len(LATE) - n_early - 1, :], M // 2, M)
-        quantize(last - 1, last)
-        quantize(last, n_pieces)
+                quantize(6, 8)
+        quantize(8, 10)
+        cast(nc.vector.tensor_copy, 11, raw_e[:, 1, :], 0, M)
+        quantize(10, 11)
+        quantize(11, 12)
+        cast(nc.vector.tensor_copy, last, raw_g[:, 0, :], M // 2, M)
+        quantize(12, 13)
+        quantize(13, 14)
 
         def picked(o, e0):
             if o == 0:
@@ -162,12 +173,12 @@ def tile_picked_deform_lin_bias_def_p_kernel(tc, x_words, x_scales, w, b, offs, 
                     lhsT=w_codes[:, u * M : (u + 1) * M].bitcast(FP8X4),
                     lhsT_scale=w_scale[:, u * M : (u + 1) * M],
                     rhs=picked(o, e0).bitcast(FP8X4),
-                    rhs_scale=x_scale[SCALE_ROWS * o :, e0 : e0 + HALF],
+                    rhs_scale=x_scale[o][:, e0 : e0 + HALF],
                     start=(u == order[0]),
                     stop=(u == order[-1]),
                 )
 
-        result = [keep.tile([M, HALF], F32, name="result%d" % h) for h in range(2)]
+        result = [keep.tile([M, HALF], F32, name="result%d" % h, align_bytes=ALIGN) for h in range(2)]
         nc.vector.tensor_scalar_add(result[0][:], acc[0][:], bias[:])
         nc.sync.dma_start(out=out[:, :HALF], in_=result[0][:])
         nc.scalar.activation(result[1][:], acc[1][:], mybir.ActivationFunctionType.Identity, bias=bias[:])

@@ -20,7 +20,7 @@ FLOPS = 2 * S * K * M
 PIECES = [(0, 0), (1, 0)] + [(o, d) for o in range(PASSES) for d in range(1, TAPS)]
 WIDE = 2 * S
 CUT_0 = [0, 4 * V, S]
-CUT_1 = [0, 4 * V, 6 * V, S]
+CUT_1 = CUT_0
 SLOT = K_PASS * 4
 
 F32 = mybir.dt.float32
@@ -41,8 +41,9 @@ def tile_picked_deform_lin_bias_def_p_kernel(tc, x_words, x_scales, w, b, offs, 
         room = ctx.enter_context(tc.tile_pool(name="room", bufs=1))
         psum = ctx.enter_context(tc.psum_pool(name="psum", bufs=1))
 
-        at_a = 0
-        at_scale = 2 * SLOT - ALIGN
+        at_single = ALIGN
+        at_a = SLOT
+        at_scale = at_a + 2 * SLOT - ALIGN
         at_b = at_scale + WIDE - ALIGN
         at_tap_0 = at_b + 2 * SLOT
         at_words_0 = at_tap_0 + 2 * SLOT
@@ -56,7 +57,7 @@ def tile_picked_deform_lin_bias_def_p_kernel(tc, x_words, x_scales, w, b, offs, 
         x_codes_0 = keep.tile([P, S], U32, name="x_codes_0", align_bytes=ALIGN)
         x_codes_1 = [keep.tile([P, CUT_1[1]], U32, name="x_codes_1_0", align_bytes=ALIGN)]
         x_scale_dense = keep.tile([P, S], U8, name="x_scale_dense", align_bytes=ALIGN)
-        x_scale = [keep.tile([P, S], U8, name="x_scale%d" % o, align_bytes=ALIGN) for o in range(PASSES)]
+        x_scale = keep.tile([P, S], U8, name="x_scale", align_bytes=ALIGN)
         w_bf = keep.tile([P, n_pieces * K_PASS], BF16, name="w_bf", align_bytes=ALIGN)
         w_codes = keep.tile([P, n_pieces * M], U32, name="w_codes", align_bytes=ALIGN)
         w_scale = keep.tile([P, n_pieces * M], U8, name="w_scale", align_bytes=ALIGN)
@@ -92,18 +93,18 @@ def tile_picked_deform_lin_bias_def_p_kernel(tc, x_words, x_scales, w, b, offs, 
         first_row = P - QUADRANT
         rows_a_pass = QUADRANTS * SCALE_ROWS
 
-        def move_scale_rows(o):
-            for r in range(SCALE_ROWS):
-                row = first_row + rows_a_pass * o + r
-                nc.sync.dma_start(
-                    out=x_scale[o][r:P:QUADRANT, :].bitcast(I32),
-                    in_=x_scale_dense[row : first_row + rows_a_pass * (o + 1) : SCALE_ROWS, :].bitcast(I32),
-                )
+        def move_scale_rows(r0, r1):
+            for r in range(r0, r1):
+                for o in range(PASSES):
+                    row = first_row + rows_a_pass * o + r
+                    nc.sync.dma_start(
+                        out=x_scale[SCALE_ROWS * o + r : P : QUADRANT, :].bitcast(I32),
+                        in_=x_scale_dense[row : first_row + rows_a_pass * (o + 1) : SCALE_ROWS, :].bitcast(I32),
+                    )
 
         nc.vector.memset(scale_win[:first_row, :T].bitcast(I32), 0)
         nc.vector.memset(scale_win[:, T:].bitcast(I32), 0)
-        for o in range(PASSES):
-            nc.vector.memset(x_scale[o][:].bitcast(I32), 0)
+        nc.vector.memset(x_scale[:].bitcast(I32), 0)
 
         nc.sync.dma_start(offsets[:], offs)
         nc.sync.dma_start(
@@ -120,9 +121,9 @@ def tile_picked_deform_lin_bias_def_p_kernel(tc, x_words, x_scales, w, b, offs, 
         for c in range(2):
             gather(x_codes_0[:, CUT_0[c] : CUT_0[c + 1]], word_win[0][:].bitcast(U32), CUT_0[c], CUT_0[c + 1])
 
-        move_scale_rows(0)
+        move_scale_rows(0, 2)
         raw_a = load_pieces(2, 2, at_a)
-        move_scale_rows(1)
+        move_scale_rows(2, 4)
         raw_b = load_pieces(4, 2, at_b)
         raw_c = load_pieces(6, 2, at_tap_0)
         raw_d = load_pieces(8, 2, at_words_0)
@@ -131,8 +132,8 @@ def tile_picked_deform_lin_bias_def_p_kernel(tc, x_words, x_scales, w, b, offs, 
             for j in range(2):
                 cast(nc.scalar.copy, u + j, raw[:, j, :], 0, M)
         cast(nc.scalar.copy, 10, raw_e[:, 0, :], 0, M)
-        raw_f = load_pieces(12, 1, at_a)
-        raw_g = load_pieces(13, 1, at_a + SLOT)
+        raw_f = load_pieces(12, 1, at_single)
+        raw_g = load_pieces(13, 1, at_single + SLOT)
         bias = room.tile([P, 1], F32, name="bias", offset=at_b + SLOT, align_bytes=ALIGN)
         nc.sync.dma_start(out=bias[:], in_=b)
         cast(nc.scalar.copy, 12, raw_f[:, 0, :], 0, M)
@@ -141,14 +142,10 @@ def tile_picked_deform_lin_bias_def_p_kernel(tc, x_words, x_scales, w, b, offs, 
         quantize(0, 2)
         gather(x_codes_1[0][:], word_win[1][:].bitcast(U32), CUT_1[0], CUT_1[1])
         quantize(2, 4)
+        x_codes_1.append(room.tile([P, S - CUT_1[1]], U32, name="x_codes_1_1", offset=at_scale, align_bytes=ALIGN))
+        gather(x_codes_1[1][:], word_win[1][:].bitcast(U32), CUT_1[1], S)
         quantize(4, 6)
-        for c, at in ((1, at_b), (2, at_tap_0)):
-            x_codes_1.append(
-                room.tile([P, CUT_1[c + 1] - CUT_1[c]], U32, name="x_codes_1_%d" % c, offset=at, align_bytes=ALIGN)
-            )
-            gather(x_codes_1[c][:], word_win[1][:].bitcast(U32), CUT_1[c], CUT_1[c + 1])
-            if c == 1:
-                quantize(6, 8)
+        quantize(6, 8)
         quantize(8, 10)
         cast(nc.vector.tensor_copy, 11, raw_e[:, 1, :], 0, M)
         quantize(10, 11)
@@ -163,7 +160,7 @@ def tile_picked_deform_lin_bias_def_p_kernel(tc, x_words, x_scales, w, b, offs, 
             c = sum(e0 >= cut for cut in CUT_1[1:])
             return x_codes_1[c][:, e0 - CUT_1[c] : e0 - CUT_1[c] + HALF]
 
-        order = [1, 0] + list(range(2, n_pieces))
+        order = list(range(n_pieces))
         for u in order:
             o, d = PIECES[u]
             for h in range(2):
@@ -173,7 +170,7 @@ def tile_picked_deform_lin_bias_def_p_kernel(tc, x_words, x_scales, w, b, offs, 
                     lhsT=w_codes[:, u * M : (u + 1) * M].bitcast(FP8X4),
                     lhsT_scale=w_scale[:, u * M : (u + 1) * M],
                     rhs=picked(o, e0).bitcast(FP8X4),
-                    rhs_scale=x_scale[o][:, e0 : e0 + HALF],
+                    rhs_scale=x_scale[SCALE_ROWS * o :, e0 : e0 + HALF],
                     start=(u == order[0]),
                     stop=(u == order[-1]),
                 )

@@ -20,7 +20,7 @@ FLOPS = 2 * S * K * M
 PIECES = [(0, 0), (1, 0)] + [(o, d) for o in range(PASSES) for d in range(1, TAPS)]
 WIDE = 2 * S
 CUT_0 = [0, 4 * V, S]
-CUT_1 = CUT_0
+CUT_1 = [0, 4 * V, 6 * V, S]
 SLOT = K_PASS * 4
 
 F32 = mybir.dt.float32
@@ -142,16 +142,18 @@ def tile_picked_deform_lin_bias_def_p_kernel(tc, x_words, x_scales, w, b, offs, 
         quantize(0, 2)
         gather(x_codes_1[0][:], word_win[1][:].bitcast(U32), CUT_1[0], CUT_1[1])
         quantize(2, 4)
-        x_codes_1.append(room.tile([P, S - CUT_1[1]], U32, name="x_codes_1_1", offset=at_scale, align_bytes=ALIGN))
-        gather(x_codes_1[1][:], word_win[1][:].bitcast(U32), CUT_1[1], S)
-        quantize(4, 6)
-        quantize(6, 8)
+        for c, at in ((1, at_scale), (2, at_b)):
+            x_codes_1.append(
+                room.tile([P, CUT_1[c + 1] - CUT_1[c]], U32, name="x_codes_1_%d" % c, offset=at, align_bytes=ALIGN)
+            )
+            gather(x_codes_1[c][:], word_win[1][:].bitcast(U32), CUT_1[c], CUT_1[c + 1])
+            quantize(2 + 2 * c, 4 + 2 * c)
         quantize(8, 10)
         cast(nc.vector.tensor_copy, 11, raw_e[:, 1, :], 0, M)
         quantize(10, 11)
         quantize(11, 12)
-        cast(nc.vector.tensor_copy, last, raw_g[:, 0, :], M // 2, M)
         quantize(12, 13)
+        cast(nc.vector.tensor_copy, last, raw_g[:, 0, :], M // 2, M)
         quantize(13, 14)
 
         def picked(o, e0):

@@ -123,8 +123,8 @@ def tile_picked_deform_lin_bias_def_p_kernel(tc, x_words, x_scales, w, b, offs, 
 
         move_scale_rows(0, 2)
         raw_a = load_pieces(2, 2, at_a)
-        move_scale_rows(2, 4)
         raw_b = load_pieces(4, 2, at_b)
+        move_scale_rows(2, 4)
         raw_c = load_pieces(6, 2, at_tap_0)
         raw_d = load_pieces(8, 2, at_words_0)
         raw_e = load_pieces(10, 2, at_words_0 + 2 * SLOT)

@@ -17,7 +17,8 @@ HALF = V // 2
 ALIGN = 256
 FLOPS = 2 * S * K * M
 
-PIECES = [(0, 0), (1, 0)] + [(o, d) for o in range(PASSES) for d in range(1, TAPS)]
+PIECES = [(o, d) for o in range(PASSES) for d in range(TAPS - 1)] + [(o, TAPS - 1) for o in range(PASSES)]
+PAIRS = (len(PIECES) - PASSES) // 2
 WIDE = 2 * S
 CUT_0 = [0, 4 * V, S]
 CUT_1 = [0, 4 * V, 6 * V, S]
@@ -36,17 +37,19 @@ def tile_picked_deform_lin_bias_def_p_kernel(tc, x_words, x_scales, w, b, offs, 
     nc = tc.nc
     n_pieces = len(PIECES)
     last = n_pieces - 1
+    first_single = 2 * PAIRS
     with ExitStack() as ctx:
         keep = ctx.enter_context(tc.tile_pool(name="keep", bufs=1))
         room = ctx.enter_context(tc.tile_pool(name="room", bufs=1))
         psum = ctx.enter_context(tc.psum_pool(name="psum", bufs=1))
 
         at_single = ALIGN
-        at_a = SLOT
-        at_scale = at_a + 2 * SLOT - ALIGN
-        at_b = at_scale + WIDE - ALIGN
-        at_tap_0 = at_b + 2 * SLOT
-        at_words_0 = at_tap_0 + 2 * SLOT
+        at_pair_1 = SLOT
+        at_scale = at_pair_1 + 2 * SLOT - ALIGN
+        at_pair_2 = at_scale + WIDE - ALIGN
+        at_pair_0 = at_pair_2 + 2 * SLOT
+        at_words_0 = at_pair_0 + 2 * SLOT
+        at_pair = [at_pair_0, at_pair_1, at_pair_2, at_pair_0, at_words_0, at_words_0 + 2 * SLOT]
 
         offsets = keep.tile([P, S // LIST_ROWS], U16, name="offsets", align_bytes=ALIGN)
         scale_win = room.tile([P, WIDE], U8, name="scale_win", offset=at_scale, align_bytes=ALIGN)
@@ -69,6 +72,9 @@ def tile_picked_deform_lin_bias_def_p_kernel(tc, x_words, x_scales, w, b, offs, 
             rows = w[d : d + n, o * K_PASS : (o + 1) * K_PASS, :]
             nc.sync.dma_start(out=raw[:], in_=rows.rearrange("d (p t) m -> p d (t m)", t=PACK))
             return raw
+
+        def load_pair(j):
+            return load_pieces(2 * j, 2, at_pair[j])
 
         def load_words(o):
             nc.sync.dma_start(out=word_win[o][:], in_=x_words[o].rearrange("p c t -> p (c t)").bitcast(I32))
@@ -111,50 +117,42 @@ def tile_picked_deform_lin_bias_def_p_kernel(tc, x_words, x_scales, w, b, offs, 
             out=scale_win[first_row:, :T].bitcast(I32), in_=x_scales.rearrange("o q c -> (o q) c").bitcast(I32)
         )
         load_words(0)
-        raw_tap_0 = room.tile([P, PASSES, K_PASS], F32, name="raw_tap_0", offset=at_tap_0, align_bytes=ALIGN)
-        nc.sync.dma_start(out=raw_tap_0[:], in_=w[0].rearrange("(o p t) m -> p o (t m)", p=P, t=PACK))
+        raw_pair = [load_pair(0)]
         load_words(1)
-        for u in range(PASSES):
-            cast(nc.scalar.copy, u, raw_tap_0[:, u, :], 0, M)
+        for u in range(2):
+            cast(nc.scalar.copy, u, raw_pair[0][:, u, :], 0, M)
 
         gather(x_scale_dense[:], scale_win[:], 0, S)
-        for c in range(2):
+        for c in range(len(CUT_0) - 1):
             gather(x_codes_0[:, CUT_0[c] : CUT_0[c + 1]], word_win[0][:].bitcast(U32), CUT_0[c], CUT_0[c + 1])
 
-        move_scale_rows(0, 2)
-        raw_a = load_pieces(2, 2, at_a)
-        raw_b = load_pieces(4, 2, at_b)
-        move_scale_rows(2, 4)
-        raw_c = load_pieces(6, 2, at_tap_0)
-        raw_d = load_pieces(8, 2, at_words_0)
-        raw_e = load_pieces(10, 2, at_words_0 + 2 * SLOT)
-        for u, raw in ((2, raw_a), (4, raw_b), (6, raw_c), (8, raw_d)):
-            for j in range(2):
-                cast(nc.scalar.copy, u + j, raw[:, j, :], 0, M)
-        cast(nc.scalar.copy, 10, raw_e[:, 0, :], 0, M)
-        raw_f = load_pieces(12, 1, at_single)
-        raw_g = load_pieces(13, 1, at_single + SLOT)
-        bias = room.tile([P, 1], F32, name="bias", offset=at_b + SLOT, align_bytes=ALIGN)
+        move_scale_rows(0, SCALE_ROWS // 2)
+        raw_pair.extend(load_pair(j) for j in (1, 2))
+        move_scale_rows(SCALE_ROWS // 2, SCALE_ROWS)
+        raw_pair.extend(load_pair(j) for j in range(3, PAIRS))
+        for u in range(2, first_single - 1):
+            cast(nc.scalar.copy, u, raw_pair[u // 2][:, u % 2, :], 0, M)
+        raw_single = [load_pieces(first_single + j, 1, at_single + j * SLOT) for j in range(PASSES)]
+        bias = room.tile([P, 1], F32, name="bias", offset=at_pair_2 + SLOT, align_bytes=ALIGN)
         nc.sync.dma_start(out=bias[:], in_=b)
-        cast(nc.scalar.copy, 12, raw_f[:, 0, :], 0, M)
-        cast(nc.scalar.copy, 13, raw_g[:, 0, :], 0, M // 2)
+        cast(nc.scalar.copy, first_single, raw_single[0][:, 0, :], 0, M)
+        cast(nc.scalar.copy, last, raw_single[1][:, 0, :], 0, M // 2)
 
         quantize(0, 2)
         gather(x_codes_1[0][:], word_win[1][:].bitcast(U32), CUT_1[0], CUT_1[1])
         quantize(2, 4)
-        for c, at in ((1, at_scale), (2, at_b)):
+        for c, at in ((1, at_scale), (2, at_pair_2)):
             x_codes_1.append(
                 room.tile([P, CUT_1[c + 1] - CUT_1[c]], U32, name="x_codes_1_%d" % c, offset=at, align_bytes=ALIGN)
             )
             gather(x_codes_1[c][:], word_win[1][:].bitcast(U32), CUT_1[c], CUT_1[c + 1])
-            quantize(2 + 2 * c, 4 + 2 * c)
-        quantize(8, 10)
-        cast(nc.vector.tensor_copy, 11, raw_e[:, 1, :], 0, M)
-        quantize(10, 11)
-        quantize(11, 12)
-        quantize(12, 13)
-        cast(nc.vector.tensor_copy, last, raw_g[:, 0, :], M // 2, M)
-        quantize(13, 14)
+            quantize(2 * (c + 1), 2 * (c + 2))
+        quantize(first_single - 4, first_single - 2)
+        cast(nc.vector.tensor_copy, first_single - 1, raw_pair[PAIRS - 1][:, 1, :], 0, M)
+        for u in range(first_single - 2, last):
+            quantize(u, u + 1)
+        cast(nc.vector.tensor_copy, last, raw_single[1][:, 0, :], M // 2, M)
+        quantize(last, n_pieces)
 
         def picked(o, e0):
             if o == 0:
@@ -162,9 +160,7 @@ def tile_picked_deform_lin_bias_def_p_kernel(tc, x_words, x_scales, w, b, offs, 
             c = sum(e0 >= cut for cut in CUT_1[1:])
             return x_codes_1[c][:, e0 - CUT_1[c] : e0 - CUT_1[c] + HALF]
 
-        order = list(range(n_pieces))
-        for u in order:
-            o, d = PIECES[u]
+        for u, (o, d) in enumerate(PIECES):
             for h in range(2):
                 e0 = d * V + h * HALF
                 nc.tensor.matmul_mx(
@@ -173,8 +169,8 @@ def tile_picked_deform_lin_bias_def_p_kernel(tc, x_words, x_scales, w, b, offs, 
                     lhsT_scale=w_scale[:, u * M : (u + 1) * M],
                     rhs=picked(o, e0).bitcast(FP8X4),
                     rhs_scale=x_scale[SCALE_ROWS * o :, e0 : e0 + HALF],
-                    start=(u == order[0]),
-                    stop=(u == order[-1]),
+                    start=(u == 0),
+                    stop=(u == last),
                 )
 
         result = [keep.tile([M, HALF], F32, name="result%d" % h, align_bytes=ALIGN) for h in range(2)]

from contextlib import ExitStack

import concourse.mybir as mybir

K, T, TAPS, V, M = 1024, 2048, 7, 256, 128
S = TAPS * V
P = 128
PACK = 4
K_PASS = P * PACK
PASSES = K // K_PASS
QUADRANT = 32
QUADRANTS = P // QUADRANT
SCALE_ROWS = 4
LIST_ROWS = 16
LINE = 4
HALF = V // 2
ALIGN = 256
FLOPS = 2 * S * K * M

PIECES = [(o, d) for o in range(PASSES) for d in range(TAPS - 1)] + [(o, TAPS - 1) for o in range(PASSES)]
PAIRS = (len(PIECES) - PASSES) // 2
WIDE = 2 * S
CUT_0 = [0, 4 * V, S]
CUT_1 = [0, 4 * V, 6 * V, S]
SLOT = K_PASS * 4

F32 = mybir.dt.float32
BF16 = mybir.dt.bfloat16
I32 = mybir.dt.int32
U32 = mybir.dt.uint32
U16 = mybir.dt.uint16
U8 = mybir.dt.uint8
FP8X4 = mybir.dt.float8_e4m3fn_x4


def tile_picked_deform_lin_bias_def_p_kernel(tc, x_words, x_scales, w, b, offs, out):
    nc = tc.nc
    n_pieces = len(PIECES)
    last = n_pieces - 1
    first_single = 2 * PAIRS
    with ExitStack() as ctx:
        keep = ctx.enter_context(tc.tile_pool(name="keep", bufs=1))
        room = ctx.enter_context(tc.tile_pool(name="room", bufs=1))
        psum = ctx.enter_context(tc.psum_pool(name="psum", bufs=1))

        at_single = ALIGN
        at_pair_1 = SLOT
        at_scale = at_pair_1 + 2 * SLOT - ALIGN
        at_pair_2 = at_scale + WIDE - ALIGN
        at_pair_0 = at_pair_2 + 2 * SLOT
        at_words_0 = at_pair_0 + 2 * SLOT
        at_pair = [at_pair_0, at_pair_1, at_pair_2, at_pair_0, at_words_0, at_words_0 + 2 * SLOT]

        offsets = keep.tile([P, S // LIST_ROWS], U16, name="offsets", align_bytes=ALIGN)
        scale_win = room.tile([P, WIDE], U8, name="scale_win", offset=at_scale, align_bytes=ALIGN)
        word_win = [
            room.tile([P, T], I32, name="word_win0", offset=at_words_0, align_bytes=ALIGN),
            keep.tile([P, T], I32, name="word_win1", align_bytes=ALIGN),
        ]
        x_codes_0 = keep.tile([P, S], U32, name="x_codes_0", align_bytes=ALIGN)
        x_codes_1 = [keep.tile([P, CUT_1[1]], U32, name="x_codes_1_0", align_bytes=ALIGN)]
        x_scale_dense = keep.tile([P, S], U8, name="x_scale_dense", align_bytes=ALIGN)
        x_scale = keep.tile([P, S], U8, name="x_scale", align_bytes=ALIGN)
        w_bf = keep.tile([P, n_pieces * K_PASS], BF16, name="w_bf", align_bytes=ALIGN)
        w_codes = keep.tile([P, n_pieces * M], U32, name="w_codes", align_bytes=ALIGN)
        w_scale = keep.tile([P, n_pieces * M], U8, name="w_scale", align_bytes=ALIGN)
        acc = [psum.tile([M, HALF], F32, name="acc%d" % h) for h in range(2)]

        def load_pieces(u, n, at):
            raw = room.tile([P, n, K_PASS], F32, name="raw%d" % u, offset=at, align_bytes=ALIGN)
            o, d = PIECES[u]
            rows = w[d : d + n, o * K_PASS : (o + 1) * K_PASS, :]
            nc.sync.dma_start(out=raw[:], in_=rows.rearrange("d (p t) m -> p d (t m)", t=PACK))
            return raw

        def load_pair(j):
            return load_pieces(2 * j, 2, at_pair[j])

        def load_words(o):
            nc.sync.dma_start(out=word_win[o][:], in_=x_words[o].rearrange("p c t -> p (c t)").bitcast(I32))

        def cast(copy, u, raw, m0, m1):
            lines = slice(m0 // LINE, m1 // LINE)
            copy(
                out=w_bf[:, u * K_PASS : (u + 1) * K_PASS].rearrange("p (c i t) -> p c t i", i=LINE, t=PACK)[:, lines],
                in_=raw.rearrange("p (t c i) -> p c t i", i=LINE, t=PACK)[:, lines],
            )

        def quantize(u0, u1):
            nc.vector.quantize_mx(
                out=w_codes[:, u0 * M : u1 * M].bitcast(FP8X4),
                scales=w_scale[:, u0 * M : u1 * M],
                in_=w_bf[:, u0 * K_PASS : u1 * K_PASS],
            )

        def gather(dst, window, e0, e1):
            nc.vector.tensor_copy(dst, window.indirect(offsets[:, e0 // LIST_ROWS : e1 // LIST_ROWS]))

        first_row = P - QUADRANT
        rows_a_pass = QUADRANTS * SCALE_ROWS

        def move_scale_rows(r0, r1):
            for r in range(r0, r1):
                for o in range(PASSES):
                    row = first_row + rows_a_pass * o + r
                    nc.sync.dma_start(
                        out=x_scale[SCALE_ROWS * o + r : P : QUADRANT, :].bitcast(I32),
                        in_=x_scale_dense[row : first_row + rows_a_pass * (o + 1) : SCALE_ROWS, :].bitcast(I32),
                    )

        nc.vector.memset(scale_win[:first_row, :T].bitcast(I32), 0)
        nc.vector.memset(scale_win[:, T:].bitcast(I32), 0)
        nc.vector.memset(x_scale[:].bitcast(I32), 0)

        nc.sync.dma_start(offsets[:], offs)
        nc.sync.dma_start(
            out=scale_win[first_row:, :T].bitcast(I32), in_=x_scales.rearrange("o q c -> (o q) c").bitcast(I32)
        )
        load_words(0)
        raw_pair = [load_pair(0)]
        load_words(1)
        for u in range(2):
            cast(nc.scalar.copy, u, raw_pair[0][:, u, :], 0, M)

        gather(x_scale_dense[:], scale_win[:], 0, S)
        for c in range(len(CUT_0) - 1):
            gather(x_codes_0[:, CUT_0[c] : CUT_0[c + 1]], word_win[0][:].bitcast(U32), CUT_0[c], CUT_0[c + 1])

        move_scale_rows(0, SCALE_ROWS // 2)
        raw_pair.extend(load_pair(j) for j in (1, 2))
        move_scale_rows(SCALE_ROWS // 2, SCALE_ROWS)
        raw_pair.extend(load_pair(j) for j in range(3, PAIRS))
        for u in range(2, first_single - 1):
            cast(nc.scalar.copy, u, raw_pair[u // 2][:, u % 2, :], 0, M)
        raw_single = [load_pieces(first_single + j, 1, at_single + j * SLOT) for j in range(PASSES)]
        bias = room.tile([P, 1], F32, name="bias", offset=at_pair_2 + SLOT, align_bytes=ALIGN)
        nc.sync.dma_start(out=bias[:], in_=b)
        cast(nc.scalar.copy, first_single, raw_single[0][:, 0, :], 0, M)
        cast(nc.scalar.copy, last, raw_single[1][:, 0, :], 0, M // 2)

        quantize(0, 2)
        gather(x_codes_1[0][:], word_win[1][:].bitcast(U32), CUT_1[0], CUT_1[1])
        quantize(2, 4)
        for c, at in ((1, at_scale), (2, at_pair_2)):
            x_codes_1.append(
                room.tile([P, CUT_1[c + 1] - CUT_1[c]], U32, name="x_codes_1_%d" % c, offset=at, align_bytes=ALIGN)
            )
            gather(x_codes_1[c][:], word_win[1][:].bitcast(U32), CUT_1[c], CUT_1[c + 1])
            quantize(2 * (c + 1), 2 * (c + 2))
        quantize(first_single - 4, first_single - 2)
        cast(nc.vector.tensor_copy, first_single - 1, raw_pair[PAIRS - 1][:, 1, :], 0, M)
        for u in range(first_single - 2, last):
            quantize(u, u + 1)
        cast(nc.vector.tensor_copy, last, raw_single[1][:, 0, :], M // 2, M)
        quantize(last, n_pieces)

        def picked(o, e0):
            if o == 0:
                return x_codes_0[:, e0 : e0 + HALF]
            c = sum(e0 >= cut for cut in CUT_1[1:])
            return x_codes_1[c][:, e0 - CUT_1[c] : e0 - CUT_1[c] + HALF]

        for u, (o, d) in enumerate(PIECES):
            for h in range(2):
                e0 = d * V + h * HALF
                nc.tensor.matmul_mx(
                    out=acc[h][:],
                    lhsT=w_codes[:, u * M : (u + 1) * M].bitcast(FP8X4),
                    lhsT_scale=w_scale[:, u * M : (u + 1) * M],
                    rhs=picked(o, e0).bitcast(FP8X4),
                    rhs_scale=x_scale[SCALE_ROWS * o :, e0 : e0 + HALF],
                    start=(u == 0),
                    stop=(u == last),
                )

        result = [keep.tile([M, HALF], F32, name="result%d" % h, align_bytes=ALIGN) for h in range(2)]
        nc.vector.tensor_scalar_add(result[0][:], acc[0][:], bias[:])
        nc.sync.dma_start(out=out[:, :HALF], in_=result[0][:])
        nc.scalar.activation(result[1][:], acc[1][:], mybir.ActivationFunctionType.Identity, bias=bias[:])
        nc.scalar.dma_start(out=out[:, HALF:], in_=result[1][:])
